import numpy as np
import ml_dtypes


def mxq(x, axis, fmt="e4m3"):
    dtype, down = {"e4m3": (ml_dtypes.float8_e4m3fn, 7), "e5m2": (ml_dtypes.float8_e5m2, 14)}[fmt]
    v = np.moveaxis(np.asarray(x, np.float32).astype(ml_dtypes.bfloat16).astype(np.float64), axis, -1)
    blocks = v.reshape(v.shape[:-1] + (-1, 32))
    amax = np.abs(blocks).max(-1, keepdims=True)
    byte = np.maximum(np.where(amax > 0, np.frexp(amax)[1] - 1 + 127, 0) - down, 1)
    scale = np.exp2(byte - 127.0)
    codes = (blocks / scale).astype(np.float32).astype(dtype).astype(np.float64)
    return np.moveaxis((codes * scale).reshape(v.shape), -1, axis)


WIDE = False


def mx_kscale(k):
    if not WIDE:
        return np.ones(k)
    levels = np.array([10, -10, 5, -5, 0])
    if k % 512:
        return np.exp2(np.random.permutation(np.resize(levels, k // 32))).repeat(32)
    a = np.empty((k // 512, 16))
    for p in range(k // 512):
        a[p, :8] = np.random.permutation(np.resize(levels, 8))
        for g in range(8):
            far = levels[np.abs(levels - a[p, g]) >= 10]
            a[p, g + 8] = far[np.random.randint(len(far))]
    return np.exp2(a.ravel()).repeat(32)


def f64(x):
    return np.asarray(x).astype(np.float64)


def striped(idx):
    return np.tile(idx.reshape(-1, 16).T, (8, 1)).astype(np.uint16)


def unstriped(offs):
    return offs[:16].T.reshape(-1).astype(np.int64)


def relu(v):
    return np.maximum(v, 0.0)


K, T, D, S, V, H, N = 512, 2048, 2, 1024, 512, 512, 256


def setup_inputs():
    n = np.random.standard_normal
    s = mx_kscale(K)[:, None]
    u = mx_kscale(H)
    return {
        "xT": (n((K, T)) * s).astype(np.float32),
        "w1": (n((K, H)) / np.sqrt(K) / s * u).astype(np.float32),
        "w2": (n((H, N)) / np.sqrt(H) / u[:, None]).astype(np.float32),
        "gate": np.tile(np.random.uniform(0.2, 1.0, (D, 1, V)) / np.sqrt(D), (1, N, 1)).astype(np.float32),
        "offs": striped(np.random.permutation(T)[:S]),
        "pos1": striped(np.random.permutation(S)[:V]),
        "pos2": striped(np.random.permutation(S)[:V]),
    }


def reference(xT, w1, w2, gate, offs, pos1, pos2):
    idx = unstriped(offs)
    xq = mxq(f64(xT)[:, idx], 0, "e4m3")
    h = relu(mxq(f64(w1), 0, "e4m3").T @ xq)
    y = mxq(f64(w2), 0, "e4m3").T @ mxq(h, 0, "e4m3")
    return sum(f64(gate[d]) * y[:, unstriped(p)] for d, p in enumerate((pos1, pos2)))

@@ -1,0 +1,248 @@
+from contextlib import ExitStack
+
+import concourse.mybir as mybir
+
+K, T, S, H, N, V = 512, 2048, 1024, 512, 256, 512
+P = 128
+
+F32 = mybir.dt.float32
+BF16 = mybir.dt.bfloat16
+U32 = mybir.dt.uint32
+U16 = mybir.dt.uint16
+U8 = mybir.dt.uint8
+FP8X4 = mybir.dt.float8_e4m3fn_x4
+
+COPY = mybir.ActivationFunctionType.Copy
+RELU = mybir.ActivationFunctionType.Relu
+MULT = mybir.AluOpType.mult
+ADD = mybir.AluOpType.add
+MAX = mybir.AluOpType.max
+
+FLOPS = 2 * S * H * K + 2 * S * N * H
+
+
+def tile_picked_sub_mlp_relu_sub_e_kernel(tc, xT, w1, w2, gate, offs, pos1, pos2, out):
+    nc = tc.nc
+    with ExitStack() as ctx:
+        keep = ctx.enter_context(tc.tile_pool(name="keep", bufs=1))
+        hbank = ctx.enter_context(tc.psum_pool(name="hbank", bufs=4))
+        ybank = ctx.enter_context(tc.psum_pool(name="ybank", bufs=1))
+
+        offs_t = keep.tile([P, S // 16], U16, name="offs_t")
+        pos_t = [keep.tile([P, V // 16], U16, name=f"pos_t{d}") for d in range(2)]
+        raw = keep.tile([P, 2, T], F32, name="raw", align_bytes=64)
+        rawp = {t: keep.tile([P, T], F32, name=f"rawp{t}", align_bytes=64) for t in (2, 3)}
+        xb = keep.tile([P, T, 2], BF16, name="xb", align_bytes=64)
+        pb = {t: keep.tile([P, T], BF16, name=f"pb{t}", align_bytes=64) for t in (2, 3)}
+        xg = keep.tile([P, S, 4], BF16, name="xg", align_bytes=64)
+        xc = keep.tile([P, S], U32, name="xc", align_bytes=64)
+        xs = keep.tile([P, S], U8, name="xs", align_bytes=64)
+        w1r = keep.tile([P, 4, H], F32, name="w1r", align_bytes=64)
+        w1g = keep.tile([P, 4, P, 4], BF16, name="w1g", align_bytes=64)
+        w1c = keep.tile([P, H], U32, name="w1c", align_bytes=64)
+        w1s = keep.tile([P, H], U8, name="w1s", align_bytes=64)
+        w2r = keep.tile([P, 4, N], F32, name="w2r", align_bytes=64)
+        w2g = keep.tile([P, N, 4], BF16, name="w2g", align_bytes=64)
+        w2c = keep.tile([P, N], U32, name="w2c", align_bytes=64)
+        w2s = keep.tile([P, N], U8, name="w2s", align_bytes=64)
+        hg = keep.tile([P, S, 4], BF16, name="hg", align_bytes=64)
+        hc = keep.tile([P, S], U32, name="hc", align_bytes=64)
+        hs = keep.tile([P, S], U8, name="hs", align_bytes=64)
+        y = [keep.tile([P, S], F32, name=f"y{m}", align_bytes=64) for m in range(2)]
+        gt = [[keep.tile([P, V], F32, name=f"gt{m}{d}", align_bytes=64) for d in range(2)] for m in range(2)]
+        part = [[keep.tile([P, V], F32, name=f"part{m}{d}", align_bytes=64) for d in range(2)] for m in range(2)]
+        res = [keep.tile([P, V], F32, name=f"res{m}", align_bytes=64) for m in range(2)]
+        warm = keep.tile([P, 8], F32, name="warm")
+
+        x4 = xT.rearrange("(p j) t -> p j t", j=4)
+        for a, b in ((0, 1024), (1024, 1536), (1536, 2048)):
+            nc.sync.dma_start(out=raw[:, :, a:b], in_=x4[:, 0:2, a:b])
+        nc.sync.dma_start(out=offs_t[:], in_=offs)
+        nc.sync.dma_start(out=rawp[2][:], in_=x4[:, 2, :])
+        nc.sync.dma_start(out=w1r[:], in_=w1.rearrange("(p j) c -> p j c", j=4))
+        for a in (0, 1024):
+            nc.sync.dma_start(out=rawp[3][:, a : a + 1024], in_=x4[:, 3, a : a + 1024])
+        w2v = w2.rearrange("(g t r) n -> t g r n", t=4, r=8)
+        for t in range(4):
+            nc.sync.dma_start(out=w2r[:, t, :], in_=w2v[t])
+        nc.sync.dma_start(out=pos_t[0][:], in_=pos1)
+        nc.sync.dma_start(out=pos_t[1][:], in_=pos2)
+        for m in range(2):
+            for d in range(2):
+                nc.sync.dma_start(out=gt[m][d][:], in_=gate[d, m * P : (m + 1) * P, :])
+
+        nc.vector.memset(warm[:], 0.0)
+        nc.scalar.activation(warm[:, 0:4], warm[:, 4:8], RELU)
+
+        def copy(engine, dst, src):
+            if engine == "s":
+                nc.scalar.copy(dst, src)
+            else:
+                nc.vector.tensor_copy(dst, src)
+
+        def cast_x(engine, u, a, b):
+            copy(engine, xb[:, a:b, :], raw[:, :, a:b].rearrange("p e t -> p t e"))
+
+        def cast_p(engine, t, a, b):
+            copy(engine, pb[t][:, a:b], rawp[t][:, a:b])
+
+        xwords = xg[:].rearrange("p n j -> p (n j)").bitcast(U32)
+        xwindow = xb[:].rearrange("p t e -> p (t e)").bitcast(U32)
+
+        def gather_x(u, a, b):
+            nc.vector.tensor_copy(xwords[:, 2 * a : 2 * b : 2], xwindow.indirect(offs_t[:, a // 16 : b // 16]))
+
+        def gather_v(t, a, b):
+            nc.vector.tensor_copy(xg[:, a:b, t], rawp[t][:].indirect(offs_t[:, a // 16 : b // 16]))
+
+        def gather_s(t, a, b):
+            nc.scalar.activation(xg[:, a:b, t], pb[t][:].indirect(offs_t[:, a // 16 : b // 16]), COPY)
+
+        def quant(codes, scales, grouped, a, b):
+            nc.vector.quantize_mx(out=codes[:, a:b].bitcast(FP8X4), scales=scales[:, a:b], in_=grouped[:, 4 * a : 4 * b])
+
+        xflat = xg[:].rearrange("p n j -> p (n j)")
+        hflat = hg[:].rearrange("p n j -> p (n j)")
+        w1src = w1r[:].rearrange("p j (g t r) -> p t g r j", t=4, r=8)
+        w1dst = w1g[:].rearrange("p t (g r) j -> p t g r j", r=8)
+        w1flat = w1g[:].rearrange("p t m j -> p (t m j)")
+        w2src = w2r[:].rearrange("p t n -> p n t")
+        w2flat = w2g[:].rearrange("p n j -> p (n j)")
+
+        def cast_w1(engine, t):
+            copy(engine, w1dst[:, t], w1src[:, t])
+
+        def cast_w2(engine, a, b):
+            copy(engine, w2g[:, a:b], w2src[:, a:b])
+
+        yb = [[ybank.tile([P, 512], F32, name=f"yb{m}{hf}") for hf in range(2)] for m in range(2)]
+        banks = {}
+
+        def layer1(c):
+            bank = hbank.tile([P, 4, P], F32, name="hb")
+            banks[c] = bank
+            for t in range(4):
+                nc.tensor.matmul_mx(
+                    out=bank[:, t, :],
+                    lhsT=w1c[:, t * P : (t + 1) * P].bitcast(FP8X4),
+                    lhsT_scale=w1s[:, t * P : (t + 1) * P],
+                    rhs=xc[:, c * P : (c + 1) * P].bitcast(FP8X4),
+                    rhs_scale=xs[:, c * P : (c + 1) * P],
+                    start=True,
+                    stop=True,
+                )
+
+        def warm_pe():
+            bank = hbank.tile([P, 4, P], F32, name="hb")
+            flat = bank[:].rearrange("p t n -> p (t n)")
+            for n in (512, 512, 256):
+                nc.tensor.matmul_mx(
+                    out=flat[:, 0:n],
+                    lhsT=w1c[:, 0:P].bitcast(FP8X4),
+                    lhsT_scale=w1s[:, 0:P],
+                    rhs=w1c[:, 0:n].bitcast(FP8X4),
+                    rhs_scale=w1s[:, 0:n],
+                    start=True,
+                    stop=True,
+                )
+
+        def relu_h(engine, c):
+            dst = hg[:, c * P : (c + 1) * P, :]
+            src = banks[c][:].rearrange("p t n -> p n t")
+            if engine == "v":
+                nc.vector.tensor_scalar(dst, src, 0.0, None, MAX)
+            else:
+                nc.scalar.activation(dst, src, RELU)
+
+        def layer2(m, a, b):
+            nc.tensor.matmul_mx(
+                out=yb[m][a // 512][:, a % 512 : a % 512 + b - a],
+                lhsT=w2c[:, m * P : (m + 1) * P].bitcast(FP8X4),
+                lhsT_scale=w2s[:, m * P : (m + 1) * P],
+                rhs=hc[:, a:b].bitcast(FP8X4),
+                rhs_scale=hs[:, a:b],
+                start=True,
+                stop=True,
+            )
+
+        def copy_y(engine, m, a, b):
+            copy(engine, y[m][:, a:b], yb[m][a // 512][:, a % 512 : a % 512 + b - a])
+
+        def gather_y(m, d, a, b):
+            idx = pos_t[d][:] if b - a == V else pos_t[d][:, a // 16 : b // 16]
+            nc.vector.tensor_tensor(part[m][d][:, a:b], y[m][:].indirect(idx), gt[m][d][:, a:b], MULT)
+
+        def finish(m, a, b):
+            nc.vector.tensor_tensor(res[m][:, a:b], part[m][0][:, a:b], part[m][1][:, a:b], ADD)
+            nc.sync.dma_start(out=out[m * P : (m + 1) * P, a:b], in_=res[m][:, a:b])
+
+        cast_x("s", 0, 0, 512)
+        cast_x("v", 0, 512, 1024)
+        cast_x("s", 0, 1024, 1280)
+        cast_x("v", 0, 1280, 1536)
+        cast_x("s", 0, 1536, 1728)
+        cast_x("v", 0, 1728, 2048)
+        gather_x(0, 0, 512)
+        gather_x(0, 512, 1024)
+        cast_p("s", 2, 0, 2048)
+        gather_v(2, 0, 512)
+        gather_s(2, 512, 1024)
+        cast_w1("v", 0)
+        cast_w1("v", 1)
+        cast_w1("v", 2)
+        cast_w1("v", 3)
+        quant(w1c, w1s, w1flat, 0, 512)
+        warm_pe()
+        cast_p("s", 3, 0, 1024)
+        cast_p("v", 3, 1024, 2048)
+        gather_v(3, 0, 256)
+        gather_v(3, 256, 512)
+        gather_s(3, 512, 768)
+        gather_s(3, 768, 1024)
+        quant(xc, xs, xflat, 0, 256)
+        quant(xc, xs, xflat, 256, 512)
+        layer1(0)
+        layer1(1)
+        layer1(2)
+        layer1(3)
+        cast_w2("s", 0, 128)
+        cast_w2("v", 128, 256)
+        relu_h("v", 0)
+        relu_h("s", 1)
+        quant(xc, xs, xflat, 512, 768)
+        quant(xc, xs, xflat, 768, 1024)
+        layer1(4)
+        layer1(5)
+        layer1(6)
+        layer1(7)
+        relu_h("s", 2)
+        relu_h("v", 3)
+        quant(w2c, w2s, w2flat, 0, 256)
+        quant(hc, hs, hflat, 0, 256)
+        relu_h("s", 4)
+        relu_h("s", 5)
+        quant(hc, hs, hflat, 256, 512)
+        layer2(0, 0, 512)
+        relu_h("v", 6)
+        relu_h("s", 7)
+        quant(hc, hs, hflat, 512, 768)
+        layer2(0, 512, 768)
+        quant(hc, hs, hflat, 768, 1024)
+        layer2(0, 768, 1024)
+        layer2(1, 0, 512)
+        layer2(1, 512, 768)
+        layer2(1, 768, 1024)
+        copy_y("s", 0, 0, 512)
+        copy_y("v", 0, 512, 768)
+        copy_y("s", 0, 768, 1024)
+        copy_y("s", 1, 0, 512)
+        copy_y("s", 1, 512, 1024)
+        gather_y(0, 0, 0, 512)
+        gather_y(0, 1, 0, 512)
+        gather_y(1, 0, 0, 384)
+        finish(0, 0, 512)
+        gather_y(1, 1, 0, 384)
+        gather_y(1, 0, 384, 512)
+        gather_y(1, 1, 384, 512)
+        finish(1, 0, 384)
+        finish(1, 384, 512)

@@ -8,71 +8,73 @@ P = 128
 F32 = mybir.dt.float32
 BF16 = mybir.dt.bfloat16
 U32 = mybir.dt.uint32
+I32 = mybir.dt.int32
 U16 = mybir.dt.uint16
 U8 = mybir.dt.uint8
 FP8X4 = mybir.dt.float8_e4m3fn_x4
 
-COPY = mybir.ActivationFunctionType.Copy
 RELU = mybir.ActivationFunctionType.Relu
+COPY = mybir.ActivationFunctionType.Copy
 MULT = mybir.AluOpType.mult
 ADD = mybir.AluOpType.add
 MAX = mybir.AluOpType.max
 
 FLOPS = 2 * S * H * K + 2 * S * N * H
 
+X_CUTS = (0, 512, 1024, 1536, 1792, 1920, 2048)
+
 
 def tile_picked_sub_mlp_relu_sub_e_kernel(tc, xT, w1, w2, gate, offs, pos1, pos2, out):
     nc = tc.nc
     with ExitStack() as ctx:
         keep = ctx.enter_context(tc.tile_pool(name="keep", bufs=1))
-        hbank = ctx.enter_context(tc.psum_pool(name="hbank", bufs=4))
-        ybank = ctx.enter_context(tc.psum_pool(name="ybank", bufs=1))
+        reuse = ctx.enter_context(tc.tile_pool(name="reuse", bufs=1))
+        psum = ctx.enter_context(tc.psum_pool(name="psum", bufs=1))
+
+        def sb(name, shape, dtype):
+            return keep.tile(shape, dtype, name=name, align_bytes=64)
 
         offs_t = keep.tile([P, S // 16], U16, name="offs_t")
         pos_t = [keep.tile([P, V // 16], U16, name=f"pos_t{d}") for d in range(2)]
-        raw = keep.tile([P, 2, T], F32, name="raw", align_bytes=64)
-        rawp = {t: keep.tile([P, T], F32, name=f"rawp{t}", align_bytes=64) for t in (2, 3)}
-        xb = keep.tile([P, T, 2], BF16, name="xb", align_bytes=64)
-        pb = {t: keep.tile([P, T], BF16, name=f"pb{t}", align_bytes=64) for t in (2, 3)}
-        xg = keep.tile([P, S, 4], BF16, name="xg", align_bytes=64)
-        xc = keep.tile([P, S], U32, name="xc", align_bytes=64)
-        xs = keep.tile([P, S], U8, name="xs", align_bytes=64)
-        w1r = keep.tile([P, 4, H], F32, name="w1r", align_bytes=64)
-        w1g = keep.tile([P, 4, P, 4], BF16, name="w1g", align_bytes=64)
-        w1c = keep.tile([P, H], U32, name="w1c", align_bytes=64)
-        w1s = keep.tile([P, H], U8, name="w1s", align_bytes=64)
-        w2r = keep.tile([P, 4, N], F32, name="w2r", align_bytes=64)
-        w2g = keep.tile([P, N, 4], BF16, name="w2g", align_bytes=64)
-        w2c = keep.tile([P, N], U32, name="w2c", align_bytes=64)
-        w2s = keep.tile([P, N], U8, name="w2s", align_bytes=64)
-        hg = keep.tile([P, S, 4], BF16, name="hg", align_bytes=64)
-        hc = keep.tile([P, S], U32, name="hc", align_bytes=64)
-        hs = keep.tile([P, S], U8, name="hs", align_bytes=64)
-        y = [keep.tile([P, S], F32, name=f"y{m}", align_bytes=64) for m in range(2)]
-        gt = [[keep.tile([P, V], F32, name=f"gt{m}{d}", align_bytes=64) for d in range(2)] for m in range(2)]
-        part = [[keep.tile([P, V], F32, name=f"part{m}{d}", align_bytes=64) for d in range(2)] for m in range(2)]
-        res = [keep.tile([P, V], F32, name=f"res{m}", align_bytes=64) for m in range(2)]
-        warm = keep.tile([P, 8], F32, name="warm")
+        chunks = list(zip(X_CUTS[:-1], X_CUTS[1:]))
+        x_raw = [sb(f"x_raw{i}", [P, 4, b - a], F32) for i, (a, b) in enumerate(chunks)]
+        x_bf = [sb(f"x_bf{i}", [P, b - a, 4], BF16) for i, (a, b) in enumerate(chunks)]
+        all_c = sb("all_c", [P, T], U32)
+        all_s = sb("all_s", [P, T], U8)
+        w1g = reuse.tile([P, 4, P, 4], BF16, name="w1g", align_bytes=64, offset=0)
+        xc = [sb(f"xc{q}", [P, 256], U32) for q in range(2)]
+        xs = [sb(f"xs{q}", [P, 256], U8) for q in range(2)]
+        xc.extend(reuse.tile([P, 256], U32, name=f"xc{q}", align_bytes=64, offset=1024 * (q - 2)) for q in (2, 3))
+        xs.extend(reuse.tile([P, 256], U8, name=f"xs{q}", align_bytes=64, offset=2048 + 256 * (q - 2)) for q in (2, 3))
+        w1r = [sb(f"w1r{u}", [P, 4, H // 2], F32) for u in range(2)]
+        w1c = sb("w1c", [P, H], U32)
+        w1s = sb("w1s", [P, H], U8)
+        w2r = reuse.tile([P, 4, N], F32, name="w2r", align_bytes=64, offset=4096)
+        w2g = sb("w2g", [P, N, 4], BF16)
+        w2c = sb("w2c", [P, N], U32)
+        w2s = sb("w2s", [P, N], U8)
+        hg = reuse.tile([P, S, 4], BF16, name="hg", align_bytes=64, offset=4096)
+        hc = sb("hc", [P, S], U32)
+        hs = sb("hs", [P, S], U8)
+        y = [sb(f"y{m}", [P, S], F32) for m in range(2)]
+        gt = sb("gt", [P, 2, V], F32)
+        part = [[sb(f"part{m}{d}", [P, V], F32) for d in range(2)] for m in range(2)]
+        res = [sb(f"res{m}", [P, V], F32) for m in range(2)]
 
         x4 = xT.rearrange("(p j) t -> p j t", j=4)
-        for a, b in ((0, 1024), (1024, 1536), (1536, 2048)):
-            nc.sync.dma_start(out=raw[:, :, a:b], in_=x4[:, 0:2, a:b])
-        nc.sync.dma_start(out=offs_t[:], in_=offs)
-        nc.sync.dma_start(out=rawp[2][:], in_=x4[:, 2, :])
-        nc.sync.dma_start(out=w1r[:], in_=w1.rearrange("(p j) c -> p j c", j=4))
-        for a in (0, 1024):
-            nc.sync.dma_start(out=rawp[3][:, a : a + 1024], in_=x4[:, 3, a : a + 1024])
-        w2v = w2.rearrange("(g t r) n -> t g r n", t=4, r=8)
-        for t in range(4):
-            nc.sync.dma_start(out=w2r[:, t, :], in_=w2v[t])
-        nc.sync.dma_start(out=pos_t[0][:], in_=pos1)
-        nc.sync.dma_start(out=pos_t[1][:], in_=pos2)
-        for m in range(2):
-            for d in range(2):
-                nc.sync.dma_start(out=gt[m][d][:], in_=gate[d, m * P : (m + 1) * P, :])
+        w14 = w1.rearrange("(p j) c -> p j c", j=4)
+        for i, (a, b) in enumerate(chunks):
+            nc.sync.dma_start(out=x_raw[i][:], in_=x4[:, :, a:b])
+            if i == 0:
+                nc.sync.dma_start(out=offs_t[:], in_=offs)
+                nc.sync.dma_start(out=pos_t[0][:], in_=pos1)
+                nc.sync.dma_start(out=pos_t[1][:], in_=pos2)
+        for u in range(2):
+            nc.sync.dma_start(out=w1r[u][:], in_=w14[:, :, u * 256 : (u + 1) * 256])
+        nc.sync.dma_start(out=w2r[:], in_=w2.rearrange("(p j) n -> p j n", j=4))
+        nc.sync.dma_start(out=gt[:], in_=gate[:, 0:P, :].rearrange("d p v -> p d v"))
 
-        nc.vector.memset(warm[:], 0.0)
-        nc.scalar.activation(warm[:, 0:4], warm[:, 4:8], RELU)
+        nc.vector.memset(all_s[:].bitcast(I32), 0)
 
         def copy(engine, dst, src):
             if engine == "s":
@@ -80,68 +82,44 @@ def tile_picked_sub_mlp_relu_sub_e_kernel(tc, xT, w1, w2, gate, offs, pos1, pos2
             else:
                 nc.vector.tensor_copy(dst, src)
 
-        def cast_x(engine, u, a, b):
-            copy(engine, xb[:, a:b, :], raw[:, :, a:b].rearrange("p e t -> p t e"))
+        def weave(engine, dst, src, a, b):
+            copy(engine, dst[:, a:b, :].rearrange("p (c i) j -> p c j i", i=4), src[:, :, a:b].rearrange("p j (c i) -> p c j i", i=4))
 
-        def cast_p(engine, t, a, b):
-            copy(engine, pb[t][:, a:b], rawp[t][:, a:b])
+        def quant(codes, scales, grouped):
+            nc.vector.quantize_mx(out=codes.bitcast(FP8X4), scales=scales, in_=grouped)
 
-        xwords = xg[:].rearrange("p n j -> p (n j)").bitcast(U32)
-        xwindow = xb[:].rearrange("p t e -> p (t e)").bitcast(U32)
+        def quant_x(i):
+            a, b = chunks[i]
+            quant(all_c[:, a:b], all_s[:, a:b], x_bf[i][:].rearrange("p n j -> p (n j)"))
 
-        def gather_x(u, a, b):
-            nc.vector.tensor_copy(xwords[:, 2 * a : 2 * b : 2], xwindow.indirect(offs_t[:, a // 16 : b // 16]))
+        def gather_x(q):
+            idx = offs_t[:, 16 * q : 16 * (q + 1)]
+            nc.vector.tensor_copy(xc[q][:], all_c[:].indirect(idx))
+            nc.vector.tensor_copy(xs[q][:], all_s[:].indirect(idx))
 
-        def gather_v(t, a, b):
-            nc.vector.tensor_copy(xg[:, a:b, t], rawp[t][:].indirect(offs_t[:, a // 16 : b // 16]))
-
-        def gather_s(t, a, b):
-            nc.scalar.activation(xg[:, a:b, t], pb[t][:].indirect(offs_t[:, a // 16 : b // 16]), COPY)
-
-        def quant(codes, scales, grouped, a, b):
-            nc.vector.quantize_mx(out=codes[:, a:b].bitcast(FP8X4), scales=scales[:, a:b], in_=grouped[:, 4 * a : 4 * b])
-
-        xflat = xg[:].rearrange("p n j -> p (n j)")
         hflat = hg[:].rearrange("p n j -> p (n j)")
-        w1src = w1r[:].rearrange("p j (g t r) -> p t g r j", t=4, r=8)
-        w1dst = w1g[:].rearrange("p t (g r) j -> p t g r j", r=8)
         w1flat = w1g[:].rearrange("p t m j -> p (t m j)")
-        w2src = w2r[:].rearrange("p t n -> p n t")
-        w2flat = w2g[:].rearrange("p n j -> p (n j)")
 
-        def cast_w1(engine, t):
-            copy(engine, w1dst[:, t], w1src[:, t])
+        def cast_w1(engine, u):
+            copy(engine, w1g[:, :, 64 * u : 64 * (u + 1), :].rearrange("p t m j -> p m j t"), w1r[u][:].rearrange("p j (m t) -> p m j t", t=4))
 
-        def cast_w2(engine, a, b):
-            copy(engine, w2g[:, a:b], w2src[:, a:b])
-
-        yb = [[ybank.tile([P, 512], F32, name=f"yb{m}{hf}") for hf in range(2)] for m in range(2)]
+        yb = {}
         banks = {}
 
+        def new_bank(b):
+            return psum.tile([P, 4, P], F32, name=f"bank{b}")
+
         def layer1(c):
-            bank = hbank.tile([P, 4, P], F32, name="hb")
+            bank = new_bank(c)
             banks[c] = bank
+            cols = slice((c % 2) * P, (c % 2 + 1) * P)
             for t in range(4):
                 nc.tensor.matmul_mx(
                     out=bank[:, t, :],
                     lhsT=w1c[:, t * P : (t + 1) * P].bitcast(FP8X4),
                     lhsT_scale=w1s[:, t * P : (t + 1) * P],
-                    rhs=xc[:, c * P : (c + 1) * P].bitcast(FP8X4),
-                    rhs_scale=xs[:, c * P : (c + 1) * P],
-                    start=True,
-                    stop=True,
-                )
-
-        def warm_pe():
-            bank = hbank.tile([P, 4, P], F32, name="hb")
-            flat = bank[:].rearrange("p t n -> p (t n)")
-            for n in (512, 512, 256):
-                nc.tensor.matmul_mx(
-                    out=flat[:, 0:n],
-                    lhsT=w1c[:, 0:P].bitcast(FP8X4),
-                    lhsT_scale=w1s[:, 0:P],
-                    rhs=w1c[:, 0:n].bitcast(FP8X4),
-                    rhs_scale=w1s[:, 0:n],
+                    rhs=xc[c // 2][:, cols].bitcast(FP8X4),
+                    rhs_scale=xs[c // 2][:, cols],
                     start=True,
                     stop=True,
                 )
@@ -154,9 +132,13 @@ def tile_picked_sub_mlp_relu_sub_e_kernel(tc, xT, w1, w2, gate, offs, pos1, pos2
             else:
                 nc.scalar.activation(dst, src, RELU)
 
-        def layer2(m, a, b):
+        def quant_h(a, b):
+            quant(hc[:, a:b], hs[:, a:b], hflat[:, 4 * a : 4 * b])
+
+        def layer2(m, a, b, bank):
+            yb[m, a] = new_bank(bank)[:].rearrange("p t n -> p (t n)")[:, 0 : b - a]
             nc.tensor.matmul_mx(
-                out=yb[m][a // 512][:, a % 512 : a % 512 + b - a],
+                out=yb[m, a],
                 lhsT=w2c[:, m * P : (m + 1) * P].bitcast(FP8X4),
                 lhsT_scale=w2s[:, m * P : (m + 1) * P],
                 rhs=hc[:, a:b].bitcast(FP8X4),
@@ -166,75 +148,50 @@ def tile_picked_sub_mlp_relu_sub_e_kernel(tc, xT, w1, w2, gate, offs, pos1, pos2
             )
 
         def copy_y(engine, m, a, b):
-            copy(engine, y[m][:, a:b], yb[m][a // 512][:, a % 512 : a % 512 + b - a])
+            copy(engine, y[m][:, a:b], yb[m, a])
 
         def gather_y(m, d, a, b):
             idx = pos_t[d][:] if b - a == V else pos_t[d][:, a // 16 : b // 16]
-            nc.vector.tensor_tensor(part[m][d][:, a:b], y[m][:].indirect(idx), gt[m][d][:, a:b], MULT)
+            nc.vector.tensor_tensor(part[m][d][:, a:b], y[m][:].indirect(idx), gt[:, d, a:b], MULT)
 
         def finish(m, a, b):
             nc.vector.tensor_tensor(res[m][:, a:b], part[m][0][:, a:b], part[m][1][:, a:b], ADD)
             nc.sync.dma_start(out=out[m * P : (m + 1) * P, a:b], in_=res[m][:, a:b])
 
-        cast_x("s", 0, 0, 512)
-        cast_x("v", 0, 512, 1024)
-        cast_x("s", 0, 1024, 1280)
-        cast_x("v", 0, 1280, 1536)
-        cast_x("s", 0, 1536, 1728)
-        cast_x("v", 0, 1728, 2048)
-        gather_x(0, 0, 512)
-        gather_x(0, 512, 1024)
-        cast_p("s", 2, 0, 2048)
-        gather_v(2, 0, 512)
-        gather_s(2, 512, 1024)
-        cast_w1("v", 0)
-        cast_w1("v", 1)
-        cast_w1("v", 2)
-        cast_w1("v", 3)
-        quant(w1c, w1s, w1flat, 0, 512)
-        warm_pe()
-        cast_p("s", 3, 0, 1024)
-        cast_p("v", 3, 1024, 2048)
-        gather_v(3, 0, 256)
-        gather_v(3, 256, 512)
-        gather_s(3, 512, 768)
-        gather_s(3, 768, 1024)
-        quant(xc, xs, xflat, 0, 256)
-        quant(xc, xs, xflat, 256, 512)
-        layer1(0)
-        layer1(1)
-        layer1(2)
-        layer1(3)
-        cast_w2("s", 0, 128)
-        cast_w2("v", 128, 256)
-        relu_h("v", 0)
-        relu_h("s", 1)
-        quant(xc, xs, xflat, 512, 768)
-        quant(xc, xs, xflat, 768, 1024)
-        layer1(4)
-        layer1(5)
-        layer1(6)
-        layer1(7)
-        relu_h("s", 2)
-        relu_h("v", 3)
-        quant(w2c, w2s, w2flat, 0, 256)
-        quant(hc, hs, hflat, 0, 256)
-        relu_h("s", 4)
-        relu_h("s", 5)
-        quant(hc, hs, hflat, 256, 512)
-        layer2(0, 0, 512)
-        relu_h("v", 6)
-        relu_h("s", 7)
-        quant(hc, hs, hflat, 512, 768)
-        layer2(0, 512, 768)
-        quant(hc, hs, hflat, 768, 1024)
-        layer2(0, 768, 1024)
-        layer2(1, 0, 512)
-        layer2(1, 512, 768)
-        layer2(1, 768, 1024)
+        for i, (a, b) in enumerate(chunks):
+            n = b - a
+            weave("s", x_bf[i], x_raw[i], 0, n // 2)
+            weave("v", x_bf[i], x_raw[i], n // 2, n)
+            if i > 0:
+                quant_x(i - 1)
+        quant_x(len(chunks) - 1)
+        cast_w1("s", 0)
+        cast_w1("s", 1)
+        gather_x(0)
+        gather_x(1)
+        quant(w1c[:], w1s[:], w1flat)
+        weave("s", w2g, w2r, 0, N)
+        for c in range(4):
+            layer1(c)
+        gather_x(2)
+        gather_x(3)
+        for c in range(4, 8):
+            layer1(c)
+        for c in range(7):
+            relu_h("s", c)
+        quant(w2c[:], w2s[:], w2g[:].rearrange("p n j -> p (n j)"))
+        quant_h(0, 512)
+        relu_h("v", 7)
+        layer2(0, 0, 512, 0)
+        quant_h(512, 768)
+        layer2(0, 512, 768, 1)
+        quant_h(768, 1024)
+        layer2(0, 768, 1024, 2)
+        layer2(1, 0, 512, 6)
+        layer2(1, 512, 1024, 7)
         copy_y("s", 0, 0, 512)
-        copy_y("v", 0, 512, 768)
-        copy_y("s", 0, 768, 1024)
+        copy_y("s", 0, 512, 768)
+        copy_y("v", 0, 768, 1024)
         copy_y("s", 1, 0, 512)
         copy_y("s", 1, 512, 1024)
         gather_y(0, 0, 0, 512)

@@ -53,10 +53,14 @@ def tile_picked_sub_mlp_relu_sub_e_kernel(tc, xT, w1, w2, gate, offs, pos1, pos2
         w2g = sb("w2g", [P, N, 4], BF16)
         w2c = sb("w2c", [P, N], U32)
         w2s = sb("w2s", [P, N], U8)
-        hg = reuse.tile([P, S, 4], BF16, name="hg", align_bytes=64, offset=4096)
+        hg = [
+            reuse.tile([P, n, 4], BF16, name=f"hg{i}", align_bytes=64, offset=at)
+            for i, (n, at) in enumerate(((512, 7168), (256, 4096), (P, 6144), (P, 7168)))
+        ]
+        h_piece = {0: (0, 0), 1: (0, 1), 2: (0, 2), 3: (0, 3), 4: (1, 0), 5: (1, 1), 6: (2, 0), 7: (3, 0)}
         hc = sb("hc", [P, S], U32)
         hs = sb("hs", [P, S], U8)
-        y = [sb(f"y{m}", [P, S], F32) for m in range(2)]
+        y = [reuse.tile([P, S], F32, name="y0", align_bytes=64, offset=6144), sb("y1", [P, S], F32)]
         gt = sb("gt", [P, 2, V], F32)
         part = [[sb(f"part{m}{d}", [P, V], F32) for d in range(2)] for m in range(2)]
         res = [sb(f"res{m}", [P, V], F32) for m in range(2)]
@@ -67,11 +71,11 @@ def tile_picked_sub_mlp_relu_sub_e_kernel(tc, xT, w1, w2, gate, offs, pos1, pos2
             nc.sync.dma_start(out=x_raw[i][:], in_=x4[:, :, a:b])
             if i == 0:
                 nc.sync.dma_start(out=offs_t[:], in_=offs)
-                nc.sync.dma_start(out=pos_t[0][:], in_=pos1)
-                nc.sync.dma_start(out=pos_t[1][:], in_=pos2)
         for u in range(2):
             nc.sync.dma_start(out=w1r[u][:], in_=w14[:, :, u * 256 : (u + 1) * 256])
         nc.sync.dma_start(out=w2r[:], in_=w2.rearrange("(p j) n -> p j n", j=4))
+        nc.sync.dma_start(out=pos_t[0][:], in_=pos1)
+        nc.sync.dma_start(out=pos_t[1][:], in_=pos2)
         nc.sync.dma_start(out=gt[:], in_=gate[:, 0:P, :].rearrange("d p v -> p d v"))
 
         nc.vector.memset(all_s[:].bitcast(I32), 0)
@@ -97,7 +101,6 @@ def tile_picked_sub_mlp_relu_sub_e_kernel(tc, xT, w1, w2, gate, offs, pos1, pos2
             nc.vector.tensor_copy(xc[q][:], all_c[:].indirect(idx))
             nc.vector.tensor_copy(xs[q][:], all_s[:].indirect(idx))
 
-        hflat = hg[:].rearrange("p n j -> p (n j)")
         w1flat = w1g[:].rearrange("p t m j -> p (t m j)")
 
         def cast_w1(engine, u):
@@ -125,7 +128,8 @@ def tile_picked_sub_mlp_relu_sub_e_kernel(tc, xT, w1, w2, gate, offs, pos1, pos2
                 )
 
         def relu_h(engine, c):
-            dst = hg[:, c * P : (c + 1) * P, :]
+            piece, i = h_piece[c]
+            dst = hg[piece][:, i * P : (i + 1) * P, :]
             src = banks[c][:].rearrange("p t n -> p n t")
             if engine == "v":
                 nc.vector.tensor_scalar(dst, src, 0.0, None, MAX)
@@ -133,7 +137,7 @@ def tile_picked_sub_mlp_relu_sub_e_kernel(tc, xT, w1, w2, gate, offs, pos1, pos2
                 nc.scalar.activation(dst, src, RELU)
 
         def quant_h(a, b):
-            quant(hc[:, a:b], hs[:, a:b], hflat[:, 4 * a : 4 * b])
+            quant(hc[:, a:b], hs[:, a:b], hg[h_piece[a // P][0]][:].rearrange("p n j -> p (n j)"))
 
         def layer2(m, a, b, bank):
             yb[m, a] = new_bank(bank)[:].rearrange("p t n -> p (t n)")[:, 0 : b - a]
@@ -181,17 +185,20 @@ def tile_picked_sub_mlp_relu_sub_e_kernel(tc, xT, w1, w2, gate, offs, pos1, pos2
             relu_h("s", c)
         quant(w2c[:], w2s[:], w2g[:].rearrange("p n j -> p (n j)"))
         quant_h(0, 512)
-        relu_h("v", 7)
         layer2(0, 0, 512, 0)
+        relu_h("v", 7)
         quant_h(512, 768)
         layer2(0, 512, 768, 1)
-        quant_h(768, 1024)
-        layer2(0, 768, 1024, 2)
-        layer2(1, 0, 512, 6)
-        layer2(1, 512, 1024, 7)
-        copy_y("s", 0, 0, 512)
+        quant_h(896, 1024)
+        layer2(0, 896, 1024, 2)
+        quant_h(768, 896)
+        layer2(0, 768, 896, 3)
+        copy_y("v", 0, 0, 512)
         copy_y("s", 0, 512, 768)
-        copy_y("v", 0, 768, 1024)
+        copy_y("s", 0, 896, 1024)
+        copy_y("s", 0, 768, 896)
+        layer2(1, 0, 512, 1)
+        layer2(1, 512, 1024, 7)
         copy_y("s", 1, 0, 512)
         copy_y("s", 1, 512, 1024)
         gather_y(0, 0, 0, 512)

@@ -43,9 +43,9 @@ def tile_picked_sub_mlp_relu_sub_e_kernel(tc, xT, w1, w2, gate, offs, pos1, pos2
         all_s = sb("all_s", [P, T], U8)
         w1g = reuse.tile([P, 4, P, 4], BF16, name="w1g", align_bytes=64, offset=0)
         xc = [sb(f"xc{q}", [P, 256], U32) for q in range(2)]
-        xs = [sb(f"xs{q}", [P, 256], U8) for q in range(2)]
+        xs = [sb("xs0", [P, 256], U8)]
         xc.extend(reuse.tile([P, 256], U32, name=f"xc{q}", align_bytes=64, offset=1024 * (q - 2)) for q in (2, 3))
-        xs.extend(reuse.tile([P, 256], U8, name=f"xs{q}", align_bytes=64, offset=2048 + 256 * (q - 2)) for q in (2, 3))
+        xs.extend(reuse.tile([P, 256], U8, name=f"xs{q}", align_bytes=64, offset=2048 + 256 * (q - 1)) for q in (1, 2, 3))
         w1r = [sb(f"w1r{u}", [P, 4, H // 2], F32) for u in range(2)]
         w1c = sb("w1c", [P, H], U32)
         w1s = sb("w1s", [P, H], U8)
@@ -96,15 +96,21 @@ def tile_picked_sub_mlp_relu_sub_e_kernel(tc, xT, w1, w2, gate, offs, pos1, pos2
             a, b = chunks[i]
             quant(all_c[:, a:b], all_s[:, a:b], x_bf[i][:].rearrange("p n j -> p (n j)"))
 
+        def gather_words(q):
+            nc.vector.tensor_copy(xc[q][:], all_c[:].indirect(offs_t[:, 16 * q : 16 * (q + 1)]))
+
+        def gather_bytes(q):
+            nc.vector.tensor_copy(xs[q][:], all_s[:].indirect(offs_t[:, 16 * q : 16 * (q + 1)]))
+
         def gather_x(q):
-            idx = offs_t[:, 16 * q : 16 * (q + 1)]
-            nc.vector.tensor_copy(xc[q][:], all_c[:].indirect(idx))
-            nc.vector.tensor_copy(xs[q][:], all_s[:].indirect(idx))
+            gather_words(q)
+            gather_bytes(q)
 
         w1flat = w1g[:].rearrange("p t m j -> p (t m j)")
 
-        def cast_w1(engine, u):
-            copy(engine, w1g[:, :, 64 * u : 64 * (u + 1), :].rearrange("p t m j -> p m j t"), w1r[u][:].rearrange("p j (m t) -> p m j t", t=4))
+        def cast_w1(engine, u, a, b):
+            dst = w1g[:, :, 64 * u + a : 64 * u + b, :].rearrange("p t m j -> p m j t")
+            copy(engine, dst, w1r[u][:, :, 4 * a : 4 * b].rearrange("p j (m t) -> p m j t", t=4))
 
         yb = {}
         banks = {}
@@ -169,11 +175,13 @@ def tile_picked_sub_mlp_relu_sub_e_kernel(tc, xT, w1, w2, gate, offs, pos1, pos2
             if i > 0:
                 quant_x(i - 1)
         quant_x(len(chunks) - 1)
-        cast_w1("s", 0)
-        cast_w1("s", 1)
+        cast_w1("s", 0, 0, 64)
+        cast_w1("s", 1, 0, 32)
         gather_x(0)
-        gather_x(1)
+        gather_words(1)
+        cast_w1("v", 1, 32, 64)
         quant(w1c[:], w1s[:], w1flat)
+        gather_bytes(1)
         weave("s", w2g, w2r, 0, N)
         for c in range(4):
             layer1(c)

@@ -60,7 +60,7 @@ def tile_picked_sub_mlp_relu_sub_e_kernel(tc, xT, w1, w2, gate, offs, pos1, pos2
         h_piece = {0: (0, 0), 1: (0, 1), 2: (0, 2), 3: (0, 3), 4: (1, 0), 5: (1, 1), 6: (2, 0), 7: (3, 0)}
         hc = sb("hc", [P, S], U32)
         hs = sb("hs", [P, S], U8)
-        y = [reuse.tile([P, S], F32, name="y0", align_bytes=64, offset=6144), sb("y1", [P, S], F32)]
+        y = [sb(f"y{m}", [P, S], F32) for m in range(2)]
         gt = sb("gt", [P, 2, V], F32)
         part = [[sb(f"part{m}{d}", [P, V], F32) for d in range(2)] for m in range(2)]
         res = [sb(f"res{m}", [P, V], F32) for m in range(2)]
@@ -111,6 +111,9 @@ def tile_picked_sub_mlp_relu_sub_e_kernel(tc, xT, w1, w2, gate, offs, pos1, pos2
         def cast_w1(engine, u, a, b):
             dst = w1g[:, :, 64 * u + a : 64 * u + b, :].rearrange("p t m j -> p m j t")
             copy(engine, dst, w1r[u][:, :, 4 * a : 4 * b].rearrange("p j (m t) -> p m j t", t=4))
+
+        def quant_w1(a, b):
+            quant(w1c[:, a * P : b * P], w1s[:, a * P : b * P], w1flat[:, 4 * a * P : 4 * b * P])
 
         yb = {}
         banks = {}
@@ -180,7 +183,8 @@ def tile_picked_sub_mlp_relu_sub_e_kernel(tc, xT, w1, w2, gate, offs, pos1, pos2
         gather_x(0)
         gather_words(1)
         cast_w1("v", 1, 32, 64)
-        quant(w1c[:], w1s[:], w1flat)
+        quant_w1(0, 2)
+        quant_w1(2, 4)
         gather_bytes(1)
         weave("s", w2g, w2r, 0, N)
         for c in range(4):
@@ -193,17 +197,19 @@ def tile_picked_sub_mlp_relu_sub_e_kernel(tc, xT, w1, w2, gate, offs, pos1, pos2
             relu_h("s", c)
         quant(w2c[:], w2s[:], w2g[:].rearrange("p n j -> p (n j)"))
         quant_h(0, 512)
-        layer2(0, 0, 512, 0)
+        layer2(0, 256, 512, 0)
         relu_h("v", 7)
         quant_h(512, 768)
         layer2(0, 512, 768, 1)
         quant_h(896, 1024)
         layer2(0, 896, 1024, 2)
         quant_h(768, 896)
+        layer2(0, 0, 256, 6)
         layer2(0, 768, 896, 3)
-        copy_y("v", 0, 0, 512)
+        copy_y("s", 0, 256, 512)
         copy_y("s", 0, 512, 768)
         copy_y("s", 0, 896, 1024)
+        copy_y("v", 0, 0, 256)
         copy_y("s", 0, 768, 896)
         layer2(1, 0, 512, 1)
         layer2(1, 512, 1024, 7)

@@ -14,14 +14,22 @@ U8 = mybir.dt.uint8
 FP8X4 = mybir.dt.float8_e4m3fn_x4
 
 RELU = mybir.ActivationFunctionType.Relu
-COPY = mybir.ActivationFunctionType.Copy
 MULT = mybir.AluOpType.mult
 ADD = mybir.AluOpType.add
 MAX = mybir.AluOpType.max
 
 FLOPS = 2 * S * H * K + 2 * S * N * H
 
-X_CUTS = (0, 512, 1024, 1536, 1792, 1920, 2048)
+SLAB_CUTS = (0, 512, 1024, 1536, 1792, 1920, 2048)
+QUARTER = S // 4
+HALF_W1 = H // 2
+LIST_ROWS = 16
+
+AT_W1 = 0
+AT_LATE_WORDS = AT_W1
+AT_LATE_BYTES = AT_W1 + 2048
+AT_W2 = 4096
+H_PIECES = ((512, AT_W2 + 3072), (256, AT_W2), (P, AT_W2 + 2048), (P, AT_W2 + 3072))
 
 
 def tile_picked_sub_mlp_relu_sub_e_kernel(tc, xT, w1, w2, gate, offs, pos1, pos2, out):
@@ -31,48 +39,51 @@ def tile_picked_sub_mlp_relu_sub_e_kernel(tc, xT, w1, w2, gate, offs, pos1, pos2
         reuse = ctx.enter_context(tc.tile_pool(name="reuse", bufs=1))
         psum = ctx.enter_context(tc.psum_pool(name="psum", bufs=1))
 
-        def sb(name, shape, dtype):
+        def own(name, shape, dtype):
             return keep.tile(shape, dtype, name=name, align_bytes=64)
 
-        offs_t = keep.tile([P, S // 16], U16, name="offs_t")
-        pos_t = [keep.tile([P, V // 16], U16, name=f"pos_t{d}") for d in range(2)]
-        chunks = list(zip(X_CUTS[:-1], X_CUTS[1:]))
-        x_raw = [sb(f"x_raw{i}", [P, 4, b - a], F32) for i, (a, b) in enumerate(chunks)]
-        x_bf = [sb(f"x_bf{i}", [P, b - a, 4], BF16) for i, (a, b) in enumerate(chunks)]
-        all_c = sb("all_c", [P, T], U32)
-        all_s = sb("all_s", [P, T], U8)
-        w1g = reuse.tile([P, 4, P, 4], BF16, name="w1g", align_bytes=64, offset=0)
-        xc = [sb(f"xc{q}", [P, 256], U32) for q in range(2)]
-        xs = [sb("xs0", [P, 256], U8)]
-        xc.extend(reuse.tile([P, 256], U32, name=f"xc{q}", align_bytes=64, offset=1024 * (q - 2)) for q in (2, 3))
-        xs.extend(reuse.tile([P, 256], U8, name=f"xs{q}", align_bytes=64, offset=2048 + 256 * (q - 1)) for q in (1, 2, 3))
-        w1r = [sb(f"w1r{u}", [P, 4, H // 2], F32) for u in range(2)]
-        w1c = sb("w1c", [P, H], U32)
-        w1s = sb("w1s", [P, H], U8)
-        w2r = reuse.tile([P, 4, N], F32, name="w2r", align_bytes=64, offset=4096)
-        w2g = sb("w2g", [P, N, 4], BF16)
-        w2c = sb("w2c", [P, N], U32)
-        w2s = sb("w2s", [P, N], U8)
-        hg = [
-            reuse.tile([P, n, 4], BF16, name=f"hg{i}", align_bytes=64, offset=at)
-            for i, (n, at) in enumerate(((512, 7168), (256, 4096), (P, 6144), (P, 7168)))
-        ]
-        h_piece = {0: (0, 0), 1: (0, 1), 2: (0, 2), 3: (0, 3), 4: (1, 0), 5: (1, 1), 6: (2, 0), 7: (3, 0)}
-        hc = sb("hc", [P, S], U32)
-        hs = sb("hs", [P, S], U8)
-        y = [sb(f"y{m}", [P, S], F32) for m in range(2)]
-        gt = sb("gt", [P, 2, V], F32)
-        part = [[sb(f"part{m}{d}", [P, V], F32) for d in range(2)] for m in range(2)]
-        res = [sb(f"res{m}", [P, V], F32) for m in range(2)]
+        def placed(name, shape, dtype, at):
+            return reuse.tile(shape, dtype, name=name, align_bytes=64, offset=at)
+
+        def take_bank(b):
+            return psum.tile([P, 4, P], F32, name=f"bank{b}")
+
+        offs_t = keep.tile([P, S // LIST_ROWS], U16, name="offs_t")
+        pos_t = [keep.tile([P, V // LIST_ROWS], U16, name=f"pos_t{d}") for d in range(2)]
+        slabs = list(zip(SLAB_CUTS[:-1], SLAB_CUTS[1:]))
+        x_raw = [own(f"x_raw{i}", [P, 4, b - a], F32) for i, (a, b) in enumerate(slabs)]
+        x_bf = [own(f"x_bf{i}", [P, b - a, 4], BF16) for i, (a, b) in enumerate(slabs)]
+        all_c = own("all_c", [P, T], U32)
+        all_s = own("all_s", [P, T], U8)
+        w1g = placed("w1g", [P, 4, P, 4], BF16, AT_W1)
+        xc = [own(f"xc{q}", [P, QUARTER], U32) for q in range(2)]
+        xs = [own("xs0", [P, QUARTER], U8)]
+        xc.extend(placed(f"xc{q}", [P, QUARTER], U32, AT_LATE_WORDS + 4 * QUARTER * (q - 2)) for q in (2, 3))
+        xs.extend(placed(f"xs{q}", [P, QUARTER], U8, AT_LATE_BYTES + QUARTER * (q - 1)) for q in (1, 2, 3))
+        w1r = [own(f"w1r{u}", [P, 4, HALF_W1], F32) for u in range(2)]
+        w1c = own("w1c", [P, H], U32)
+        w1s = own("w1s", [P, H], U8)
+        w2r = placed("w2r", [P, 4, N], F32, AT_W2)
+        w2g = own("w2g", [P, N, 4], BF16)
+        w2c = own("w2c", [P, N], U32)
+        w2s = own("w2s", [P, N], U8)
+        hg = [placed(f"hg{i}", [P, n, 4], BF16, at) for i, (n, at) in enumerate(H_PIECES)]
+        h_place = [(i, nth) for i, (n, at) in enumerate(H_PIECES) for nth in range(n // P)]
+        hc = own("hc", [P, S], U32)
+        hs = own("hs", [P, S], U8)
+        y = [own(f"y{m}", [P, S], F32) for m in range(2)]
+        gt = own("gt", [P, 2, V], F32)
+        part = [[own(f"part{m}{d}", [P, V], F32) for d in range(2)] for m in range(2)]
+        res = [own(f"res{m}", [P, V], F32) for m in range(2)]
 
         x4 = xT.rearrange("(p j) t -> p j t", j=4)
         w14 = w1.rearrange("(p j) c -> p j c", j=4)
-        for i, (a, b) in enumerate(chunks):
+        for i, (a, b) in enumerate(slabs):
             nc.sync.dma_start(out=x_raw[i][:], in_=x4[:, :, a:b])
             if i == 0:
                 nc.sync.dma_start(out=offs_t[:], in_=offs)
         for u in range(2):
-            nc.sync.dma_start(out=w1r[u][:], in_=w14[:, :, u * 256 : (u + 1) * 256])
+            nc.sync.dma_start(out=w1r[u][:], in_=w14[:, :, u * HALF_W1 : (u + 1) * HALF_W1])
         nc.sync.dma_start(out=w2r[:], in_=w2.rearrange("(p j) n -> p j n", j=4))
         nc.sync.dma_start(out=pos_t[0][:], in_=pos1)
         nc.sync.dma_start(out=pos_t[1][:], in_=pos2)
@@ -81,53 +92,54 @@ def tile_picked_sub_mlp_relu_sub_e_kernel(tc, xT, w1, w2, gate, offs, pos1, pos2
         nc.vector.memset(all_s[:].bitcast(I32), 0)
 
         def copy(engine, dst, src):
-            if engine == "s":
+            if engine == "scalar":
                 nc.scalar.copy(dst, src)
             else:
                 nc.vector.tensor_copy(dst, src)
 
         def weave(engine, dst, src, a, b):
-            copy(engine, dst[:, a:b, :].rearrange("p (c i) j -> p c j i", i=4), src[:, :, a:b].rearrange("p j (c i) -> p c j i", i=4))
+            copy(
+                engine,
+                dst[:, a:b, :].rearrange("p (c i) j -> p c j i", i=4),
+                src[:, :, a:b].rearrange("p j (c i) -> p c j i", i=4),
+            )
 
-        def quant(codes, scales, grouped):
-            nc.vector.quantize_mx(out=codes.bitcast(FP8X4), scales=scales, in_=grouped)
-
-        def quant_x(i):
-            a, b = chunks[i]
-            quant(all_c[:, a:b], all_s[:, a:b], x_bf[i][:].rearrange("p n j -> p (n j)"))
-
-        def gather_words(q):
-            nc.vector.tensor_copy(xc[q][:], all_c[:].indirect(offs_t[:, 16 * q : 16 * (q + 1)]))
-
-        def gather_bytes(q):
-            nc.vector.tensor_copy(xs[q][:], all_s[:].indirect(offs_t[:, 16 * q : 16 * (q + 1)]))
-
-        def gather_x(q):
-            gather_words(q)
-            gather_bytes(q)
-
-        w1flat = w1g[:].rearrange("p t m j -> p (t m j)")
-
-        def cast_w1(engine, u, a, b):
+        def weave_w1(engine, u, a, b):
             dst = w1g[:, :, 64 * u + a : 64 * u + b, :].rearrange("p t m j -> p m j t")
             copy(engine, dst, w1r[u][:, :, 4 * a : 4 * b].rearrange("p j (m t) -> p m j t", t=4))
 
-        def quant_w1(a, b):
-            quant(w1c[:, a * P : b * P], w1s[:, a * P : b * P], w1flat[:, 4 * a * P : 4 * b * P])
+        def quant(words, scales, woven):
+            nc.vector.quantize_mx(out=words.bitcast(FP8X4), scales=scales, in_=woven)
 
-        yb = {}
-        banks = {}
+        def quant_slab(i):
+            a, b = slabs[i]
+            quant(all_c[:, a:b], all_s[:, a:b], x_bf[i][:].rearrange("p n j -> p (n j)"))
 
-        def new_bank(b):
-            return psum.tile([P, 4, P], F32, name=f"bank{b}")
+        def quant_w1(t0, t1):
+            flat = w1g[:].rearrange("p t m j -> p (t m j)")
+            quant(w1c[:, t0 * P : t1 * P], w1s[:, t0 * P : t1 * P], flat[:, 4 * t0 * P : 4 * t1 * P])
+
+        def quant_h(a, b):
+            quant(hc[:, a:b], hs[:, a:b], hg[h_place[a // P][0]][:].rearrange("p n j -> p (n j)"))
+
+        def entries(list_tile, a, b):
+            return list_tile[:, a // LIST_ROWS : b // LIST_ROWS]
+
+        def gather_words(q):
+            nc.vector.tensor_copy(xc[q][:], all_c[:].indirect(entries(offs_t, q * QUARTER, (q + 1) * QUARTER)))
+
+        def gather_bytes(q):
+            nc.vector.tensor_copy(xs[q][:], all_s[:].indirect(entries(offs_t, q * QUARTER, (q + 1) * QUARTER)))
+
+        h_bank = {}
+        y_bank = {}
 
         def layer1(c):
-            bank = new_bank(c)
-            banks[c] = bank
+            h_bank[c] = take_bank(c)
             cols = slice((c % 2) * P, (c % 2 + 1) * P)
             for t in range(4):
                 nc.tensor.matmul_mx(
-                    out=bank[:, t, :],
+                    out=h_bank[c][:, t, :],
                     lhsT=w1c[:, t * P : (t + 1) * P].bitcast(FP8X4),
                     lhsT_scale=w1s[:, t * P : (t + 1) * P],
                     rhs=xc[c // 2][:, cols].bitcast(FP8X4),
@@ -136,22 +148,19 @@ def tile_picked_sub_mlp_relu_sub_e_kernel(tc, xT, w1, w2, gate, offs, pos1, pos2
                     stop=True,
                 )
 
-        def relu_h(engine, c):
-            piece, i = h_piece[c]
-            dst = hg[piece][:, i * P : (i + 1) * P, :]
-            src = banks[c][:].rearrange("p t n -> p n t")
-            if engine == "v":
-                nc.vector.tensor_scalar(dst, src, 0.0, None, MAX)
-            else:
+        def relu_out(engine, c):
+            piece, nth = h_place[c]
+            dst = hg[piece][:, nth * P : (nth + 1) * P, :]
+            src = h_bank[c][:].rearrange("p t n -> p n t")
+            if engine == "scalar":
                 nc.scalar.activation(dst, src, RELU)
-
-        def quant_h(a, b):
-            quant(hc[:, a:b], hs[:, a:b], hg[h_piece[a // P][0]][:].rearrange("p n j -> p (n j)"))
+            else:
+                nc.vector.tensor_scalar(dst, src, 0.0, None, MAX)
 
         def layer2(m, a, b, bank):
-            yb[m, a] = new_bank(bank)[:].rearrange("p t n -> p (t n)")[:, 0 : b - a]
+            y_bank[m, a] = take_bank(bank)[:].rearrange("p t n -> p (t n)")[:, 0 : b - a]
             nc.tensor.matmul_mx(
-                out=yb[m, a],
+                out=y_bank[m, a],
                 lhsT=w2c[:, m * P : (m + 1) * P].bitcast(FP8X4),
                 lhsT_scale=w2s[:, m * P : (m + 1) * P],
                 rhs=hc[:, a:b].bitcast(FP8X4),
@@ -160,45 +169,49 @@ def tile_picked_sub_mlp_relu_sub_e_kernel(tc, xT, w1, w2, gate, offs, pos1, pos2
                 stop=True,
             )
 
-        def copy_y(engine, m, a, b):
-            copy(engine, y[m][:, a:b], yb[m, a])
+        def y_out(engine, m, a, b):
+            copy(engine, y[m][:, a:b], y_bank[m, a])
 
-        def gather_y(m, d, a, b):
-            idx = pos_t[d][:] if b - a == V else pos_t[d][:, a // 16 : b // 16]
-            nc.vector.tensor_tensor(part[m][d][:, a:b], y[m][:].indirect(idx), gt[:, d, a:b], MULT)
+        def fetch(m, d, a, b):
+            nc.vector.tensor_tensor(part[m][d][:, a:b], y[m][:].indirect(entries(pos_t[d], a, b)), gt[:, d, a:b], MULT)
 
         def finish(m, a, b):
             nc.vector.tensor_tensor(res[m][:, a:b], part[m][0][:, a:b], part[m][1][:, a:b], ADD)
             nc.sync.dma_start(out=out[m * P : (m + 1) * P, a:b], in_=res[m][:, a:b])
 
-        for i, (a, b) in enumerate(chunks):
+        for i, (a, b) in enumerate(slabs):
             n = b - a
-            weave("s", x_bf[i], x_raw[i], 0, n // 2)
-            weave("v", x_bf[i], x_raw[i], n // 2, n)
+            weave("scalar", x_bf[i], x_raw[i], 0, n // 2)
+            weave("vector", x_bf[i], x_raw[i], n // 2, n)
             if i > 0:
-                quant_x(i - 1)
-        quant_x(len(chunks) - 1)
-        cast_w1("s", 0, 0, 64)
-        cast_w1("s", 1, 0, 32)
-        gather_x(0)
+                quant_slab(i - 1)
+        quant_slab(len(slabs) - 1)
+
+        weave_w1("scalar", 0, 0, 64)
+        weave_w1("scalar", 1, 0, 32)
+        gather_words(0)
+        gather_bytes(0)
         gather_words(1)
-        cast_w1("v", 1, 32, 64)
+        weave_w1("vector", 1, 32, 64)
         quant_w1(0, 2)
         quant_w1(2, 4)
         gather_bytes(1)
-        weave("s", w2g, w2r, 0, N)
+        weave("scalar", w2g, w2r, 0, N)
+
         for c in range(4):
             layer1(c)
-        gather_x(2)
-        gather_x(3)
+        for q in (2, 3):
+            gather_words(q)
+            gather_bytes(q)
         for c in range(4, 8):
             layer1(c)
         for c in range(7):
-            relu_h("s", c)
+            relu_out("scalar", c)
         quant(w2c[:], w2s[:], w2g[:].rearrange("p n j -> p (n j)"))
+
         quant_h(0, 512)
         layer2(0, 256, 512, 0)
-        relu_h("v", 7)
+        relu_out("vector", 7)
         quant_h(512, 768)
         layer2(0, 512, 768, 1)
         quant_h(896, 1024)
@@ -206,21 +219,21 @@ def tile_picked_sub_mlp_relu_sub_e_kernel(tc, xT, w1, w2, gate, offs, pos1, pos2
         quant_h(768, 896)
         layer2(0, 0, 256, 6)
         layer2(0, 768, 896, 3)
-        copy_y("s", 0, 256, 512)
-        copy_y("s", 0, 512, 768)
-        copy_y("s", 0, 896, 1024)
-        copy_y("v", 0, 0, 256)
-        copy_y("s", 0, 768, 896)
+        y_out("scalar", 0, 256, 512)
+        y_out("scalar", 0, 512, 768)
+        y_out("scalar", 0, 896, 1024)
+        y_out("vector", 0, 0, 256)
+        y_out("scalar", 0, 768, 896)
         layer2(1, 0, 512, 1)
         layer2(1, 512, 1024, 7)
-        copy_y("s", 1, 0, 512)
-        copy_y("s", 1, 512, 1024)
-        gather_y(0, 0, 0, 512)
-        gather_y(0, 1, 0, 512)
-        gather_y(1, 0, 0, 384)
-        finish(0, 0, 512)
-        gather_y(1, 1, 0, 384)
-        gather_y(1, 0, 384, 512)
-        gather_y(1, 1, 384, 512)
-        finish(1, 0, 384)
-        finish(1, 384, 512)
+        y_out("scalar", 1, 0, 512)
+        y_out("scalar", 1, 512, 1024)
+
+        fetch(0, 0, 0, V)
+        fetch(0, 1, 0, V)
+        fetch(1, 0, 0, V)
+        finish(0, 0, V)
+        fetch(1, 1, 0, V // 2)
+        fetch(1, 1, V // 2, V)
+        finish(1, 0, V // 2)
+        finish(1, V // 2, V)

@@ -1,6 +1,7 @@
 from contextlib import ExitStack
 
 import concourse.mybir as mybir
+from concourse.masks import make_identity
 
 K, T, S, H, N, V = 512, 2048, 1024, 512, 256, 512
 P = 128
@@ -75,6 +76,9 @@ def tile_picked_sub_mlp_relu_sub_e_kernel(tc, xT, w1, w2, gate, offs, pos1, pos2
         gt = own("gt", [P, 2, V], F32)
         part = [[own(f"part{m}{d}", [P, V], F32) for d in range(2)] for m in range(2)]
         res = [own(f"res{m}", [P, V], F32) for m in range(2)]
+        ident = own("ident", [P, P], F32)
+        turned_sum = own("turned_sum", [P, 4, P], F32)
+        make_identity(nc, ident[:])
 
         x4 = xT.rearrange("(p j) t -> p j t", j=4)
         w14 = w1.rearrange("(p j) c -> p j c", j=4)
@@ -230,9 +234,27 @@ def tile_picked_sub_mlp_relu_sub_e_kernel(tc, xT, w1, w2, gate, offs, pos1, pos2
         y_out("scalar", 1, 512, 1024)
 
         fetch(0, 0, 0, V)
-        fetch(0, 1, 0, V)
+        fetch(0, 1, 0, V // 2)
+        fetch(0, 1, V // 2, V)
         fetch(1, 0, 0, V)
-        finish(0, 0, V)
+        turned = [take_bank(b) for b in (2, 3, 4, 5)]
+        for d in range(2):
+            for k in range(4):
+                nc.tensor.matmul(
+                    turned[k][:, 0, :],
+                    part[0][d][:, k * P : (k + 1) * P],
+                    ident[:],
+                    start=(d == 0),
+                    stop=(d == 1),
+                    is_transpose=True,
+                )
+        back = [take_bank(b) for b in (0, 6)]
+        for k in range(4):
+            nc.scalar.copy(turned_sum[:, k, :], turned[k][:, 0, :])
+            nc.tensor.transpose(back[k // 2][:, k % 2, :], turned_sum[:, k, :], ident[:])
+        for u in range(2):
+            nc.scalar.copy(res[0][:, 2 * u * P : 2 * (u + 1) * P], back[u][:, 0:2, :].rearrange("p t n -> p (t n)"))
+        nc.scalar.dma_start(out=out[0:P, :], in_=res[0][:])
         fetch(1, 1, 0, V // 2)
         fetch(1, 1, V // 2, V)
         finish(1, 0, V // 2)

@@ -21,16 +21,17 @@ MAX = mybir.AluOpType.max
 
 FLOPS = 2 * S * H * K + 2 * S * N * H
 
-SLAB_CUTS = (0, 512, 1024, 1536, 1792, 1920, 2048)
+SLAB_CUTS = (0, 640, 1280, 1664, 1920, 2048)
+SCALAR_SHARE = (224, 224, 128, 96, 64)
 QUARTER = S // 4
-HALF_W1 = H // 2
+W1_CUTS = (0, 192, 384, 512)
 LIST_ROWS = 16
 
 AT_W1 = 0
 AT_LATE_WORDS = AT_W1
 AT_LATE_BYTES = AT_W1 + 2048
 AT_W2 = 4096
-H_PIECES = ((512, AT_W2 + 3072), (256, AT_W2), (P, AT_W2 + 2048), (P, AT_W2 + 3072))
+H_PIECES = ((512, AT_W2 + 3072), (256, AT_W2), (P, AT_W2 + 2048), (P, AT_W2))
 
 
 def tile_picked_sub_mlp_relu_sub_e_kernel(tc, xT, w1, w2, gate, offs, pos1, pos2, out):
@@ -58,10 +59,11 @@ def tile_picked_sub_mlp_relu_sub_e_kernel(tc, xT, w1, w2, gate, offs, pos1, pos2
         all_s = own("all_s", [P, T], U8)
         w1g = placed("w1g", [P, 4, P, 4], BF16, AT_W1)
         xc = [own(f"xc{q}", [P, QUARTER], U32) for q in range(2)]
-        xs = [own("xs0", [P, QUARTER], U8)]
+        xs = [own(f"xs{q}", [P, QUARTER], U8) for q in range(2)]
         xc.extend(placed(f"xc{q}", [P, QUARTER], U32, AT_LATE_WORDS + 4 * QUARTER * (q - 2)) for q in (2, 3))
-        xs.extend(placed(f"xs{q}", [P, QUARTER], U8, AT_LATE_BYTES + QUARTER * (q - 1)) for q in (1, 2, 3))
-        w1r = [own(f"w1r{u}", [P, 4, HALF_W1], F32) for u in range(2)]
+        xs.extend(placed(f"xs{q}", [P, QUARTER], U8, AT_LATE_BYTES + QUARTER * (q - 2)) for q in (2, 3))
+        w1_parts = list(zip(W1_CUTS[:-1], W1_CUTS[1:]))
+        w1r = [own(f"w1r{u}", [P, 4, b - a], F32) for u, (a, b) in enumerate(w1_parts)]
         w1c = own("w1c", [P, H], U32)
         w1s = own("w1s", [P, H], U8)
         w2r = placed("w2r", [P, 4, N], F32, AT_W2)
@@ -86,8 +88,8 @@ def tile_picked_sub_mlp_relu_sub_e_kernel(tc, xT, w1, w2, gate, offs, pos1, pos2
             nc.sync.dma_start(out=x_raw[i][:], in_=x4[:, :, a:b])
             if i == 0:
                 nc.sync.dma_start(out=offs_t[:], in_=offs)
-        for u in range(2):
-            nc.sync.dma_start(out=w1r[u][:], in_=w14[:, :, u * HALF_W1 : (u + 1) * HALF_W1])
+        for u, (a, b) in enumerate(w1_parts):
+            nc.sync.dma_start(out=w1r[u][:], in_=w14[:, :, a:b])
         nc.sync.dma_start(out=w2r[:], in_=w2.rearrange("(p j) n -> p j n", j=4))
         nc.sync.dma_start(out=pos_t[0][:], in_=pos1)
         nc.sync.dma_start(out=pos_t[1][:], in_=pos2)
@@ -108,16 +110,20 @@ def tile_picked_sub_mlp_relu_sub_e_kernel(tc, xT, w1, w2, gate, offs, pos1, pos2
                 src[:, :, a:b].rearrange("p j (c i) -> p c j i", i=4),
             )
 
-        def weave_w1(engine, u, a, b):
-            dst = w1g[:, :, 64 * u + a : 64 * u + b, :].rearrange("p t m j -> p m j t")
-            copy(engine, dst, w1r[u][:, :, 4 * a : 4 * b].rearrange("p j (m t) -> p m j t", t=4))
+        def weave_w1(u):
+            a, b = w1_parts[u]
+            dst = w1g[:, :, a // 4 : b // 4, :].rearrange("p t m j -> p m j t")
+            nc.scalar.copy(dst, w1r[u][:].rearrange("p j (m t) -> p m j t", t=4))
 
         def quant(words, scales, woven):
             nc.vector.quantize_mx(out=words.bitcast(FP8X4), scales=scales, in_=woven)
 
         def quant_slab(i):
             a, b = slabs[i]
-            quant(all_c[:, a:b], all_s[:, a:b], x_bf[i][:].rearrange("p n j -> p (n j)"))
+            flat = x_bf[i][:].rearrange("p n j -> p (n j)")
+            cuts = (0, b - a) if b - a in (128, 256, 512) else (0, P, b - a)
+            for lo, hi in zip(cuts[:-1], cuts[1:]):
+                quant(all_c[:, a + lo : a + hi], all_s[:, a + lo : a + hi], flat[:, 4 * lo : 4 * hi])
 
         def quant_w1(t0, t1):
             flat = w1g[:].rearrange("p t m j -> p (t m j)")
@@ -185,21 +191,19 @@ def tile_picked_sub_mlp_relu_sub_e_kernel(tc, xT, w1, w2, gate, offs, pos1, pos2
 
         for i, (a, b) in enumerate(slabs):
             n = b - a
-            weave("scalar", x_bf[i], x_raw[i], 0, n // 2)
-            weave("vector", x_bf[i], x_raw[i], n // 2, n)
+            weave("scalar", x_bf[i], x_raw[i], 0, SCALAR_SHARE[i])
+            weave("vector", x_bf[i], x_raw[i], SCALAR_SHARE[i], n)
             if i > 0:
                 quant_slab(i - 1)
         quant_slab(len(slabs) - 1)
 
-        weave_w1("scalar", 0, 0, 64)
-        weave_w1("scalar", 1, 0, 32)
-        gather_words(0)
-        gather_bytes(0)
-        gather_words(1)
-        weave_w1("vector", 1, 32, 64)
+        for u in range(len(w1_parts)):
+            weave_w1(u)
+        for q in (0, 1):
+            gather_words(q)
+            gather_bytes(q)
         quant_w1(0, 2)
         quant_w1(2, 4)
-        gather_bytes(1)
         weave("scalar", w2g, w2r, 0, N)
 
         for c in range(4):
@@ -209,27 +213,26 @@ def tile_picked_sub_mlp_relu_sub_e_kernel(tc, xT, w1, w2, gate, offs, pos1, pos2
             gather_bytes(q)
         for c in range(4, 8):
             layer1(c)
-        for c in range(7):
+        for c in (0, 1, 2, 3, 5, 6):
             relu_out("scalar", c)
         quant(w2c[:], w2s[:], w2g[:].rearrange("p n j -> p (n j)"))
 
+        relu_out("vector", 4)
         quant_h(0, 512)
-        layer2(0, 256, 512, 0)
-        relu_out("vector", 7)
+        layer2(0, 0, 512, 0)
         quant_h(512, 768)
         layer2(0, 512, 768, 1)
-        quant_h(896, 1024)
-        layer2(0, 896, 1024, 2)
+        relu_out("vector", 7)
         quant_h(768, 896)
-        layer2(0, 0, 256, 6)
-        layer2(0, 768, 896, 3)
-        y_out("scalar", 0, 256, 512)
+        layer2(0, 768, 896, 2)
+        quant_h(896, 1024)
+        layer2(0, 896, 1024, 3)
+        y_out("scalar", 0, 0, 512)
         y_out("scalar", 0, 512, 768)
-        y_out("scalar", 0, 896, 1024)
-        y_out("vector", 0, 0, 256)
         y_out("scalar", 0, 768, 896)
-        layer2(1, 0, 512, 1)
-        layer2(1, 512, 1024, 7)
+        y_out("scalar", 0, 896, 1024)
+        layer2(1, 0, 512, 2)
+        layer2(1, 512, 1024, 3)
         y_out("scalar", 1, 0, 512)
         y_out("scalar", 1, 512, 1024)
 
@@ -237,7 +240,7 @@ def tile_picked_sub_mlp_relu_sub_e_kernel(tc, xT, w1, w2, gate, offs, pos1, pos2
         fetch(0, 1, 0, V // 2)
         fetch(0, 1, V // 2, V)
         fetch(1, 0, 0, V)
-        turned = [take_bank(b) for b in (2, 3, 4, 5)]
+        turned = [take_bank(b) for b in (4, 5, 6, 7)]
         for d in range(2):
             for k in range(4):
                 nc.tensor.matmul(
@@ -248,7 +251,7 @@ def tile_picked_sub_mlp_relu_sub_e_kernel(tc, xT, w1, w2, gate, offs, pos1, pos2
                     stop=(d == 1),
                     is_transpose=True,
                 )
-        back = [take_bank(b) for b in (0, 6)]
+        back = [take_bank(b) for b in (0, 1)]
         for k in range(4):
             nc.scalar.copy(turned_sum[:, k, :], turned[k][:, 0, :])
             nc.tensor.transpose(back[k // 2][:, k % 2, :], turned_sum[:, k, :], ident[:])

@@ -9,11 +9,11 @@ P = 128
 F32 = mybir.dt.float32
 BF16 = mybir.dt.bfloat16
 U32 = mybir.dt.uint32
-I32 = mybir.dt.int32
 U16 = mybir.dt.uint16
 U8 = mybir.dt.uint8
 FP8X4 = mybir.dt.float8_e4m3fn_x4
 
+COPY = mybir.ActivationFunctionType.Copy
 RELU = mybir.ActivationFunctionType.Relu
 MULT = mybir.AluOpType.mult
 ADD = mybir.AluOpType.add
@@ -21,17 +21,17 @@ MAX = mybir.AluOpType.max
 
 FLOPS = 2 * S * H * K + 2 * S * N * H
 
-SLAB_CUTS = (0, 640, 1280, 1664, 1920, 2048)
-SCALAR_SHARE = (224, 224, 128, 96, 64)
-QUARTER = S // 4
-W1_CUTS = (0, 192, 384, 512)
+PLANE_ORDER = (0, 2, 1, 3)
+SCALAR_ENTRIES = 256
+LIST_CUTS = (0, 256, 512, 1024)
+W1_CUTS = (0, 160, 352, 512)
 LIST_ROWS = 16
 
 AT_W1 = 0
-AT_LATE_WORDS = AT_W1
-AT_LATE_BYTES = AT_W1 + 2048
-AT_W2 = 4096
-H_PIECES = ((512, AT_W2 + 3072), (256, AT_W2), (P, AT_W2 + 2048), (P, AT_W2))
+AT_XC1 = AT_W1
+AT_XG2 = AT_W1 + 1024
+AT_W2 = 5120
+H_PIECES = ((512, AT_W2 + 3072), (256, AT_W2), (P, AT_W2 + 2048), (P, AT_W2 + 7168))
 
 
 def tile_picked_sub_mlp_relu_sub_e_kernel(tc, xT, w1, w2, gate, offs, pos1, pos2, out):
@@ -52,16 +52,14 @@ def tile_picked_sub_mlp_relu_sub_e_kernel(tc, xT, w1, w2, gate, offs, pos1, pos2
 
         offs_t = keep.tile([P, S // LIST_ROWS], U16, name="offs_t")
         pos_t = [keep.tile([P, V // LIST_ROWS], U16, name=f"pos_t{d}") for d in range(2)]
-        slabs = list(zip(SLAB_CUTS[:-1], SLAB_CUTS[1:]))
-        x_raw = [own(f"x_raw{i}", [P, 4, b - a], F32) for i, (a, b) in enumerate(slabs)]
-        x_bf = [own(f"x_bf{i}", [P, b - a, 4], BF16) for i, (a, b) in enumerate(slabs)]
-        all_c = own("all_c", [P, T], U32)
-        all_s = own("all_s", [P, T], U8)
+        plane = [own(f"plane{j}", [P, T], F32) for j in range(4)]
+        plane_bf = [own(f"plane_bf{j}", [P, T], BF16) for j in range(2)]
+        pairs = own("pairs", [P, 2, S, 2], BF16)
         w1g = placed("w1g", [P, 4, P, 4], BF16, AT_W1)
-        xc = [own(f"xc{q}", [P, QUARTER], U32) for q in range(2)]
-        xs = [own(f"xs{q}", [P, QUARTER], U8) for q in range(2)]
-        xc.extend(placed(f"xc{q}", [P, QUARTER], U32, AT_LATE_WORDS + 4 * QUARTER * (q - 2)) for q in (2, 3))
-        xs.extend(placed(f"xs{q}", [P, QUARTER], U8, AT_LATE_BYTES + QUARTER * (q - 2)) for q in (2, 3))
+        picks = list(zip(LIST_CUTS[:-1], LIST_CUTS[1:]))
+        xg = [own("xg0", [P, 256, 4], BF16), own("xg1", [P, 256, 4], BF16), placed("xg2", [P, 512, 4], BF16, AT_XG2)]
+        xc = [own("xc0", [P, 256], U32), placed("xc1", [P, 256], U32, AT_XC1), own("xc2", [P, 512], U32)]
+        xs = [own(f"xs{q}", [P, b - a], U8) for q, (a, b) in enumerate(picks)]
         w1_parts = list(zip(W1_CUTS[:-1], W1_CUTS[1:]))
         w1r = [own(f"w1r{u}", [P, 4, b - a], F32) for u, (a, b) in enumerate(w1_parts)]
         w1c = own("w1c", [P, H], U32)
@@ -84,9 +82,9 @@ def tile_picked_sub_mlp_relu_sub_e_kernel(tc, xT, w1, w2, gate, offs, pos1, pos2
 
         x4 = xT.rearrange("(p j) t -> p j t", j=4)
         w14 = w1.rearrange("(p j) c -> p j c", j=4)
-        for i, (a, b) in enumerate(slabs):
-            nc.sync.dma_start(out=x_raw[i][:], in_=x4[:, :, a:b])
-            if i == 0:
+        for j in PLANE_ORDER:
+            nc.sync.dma_start(out=plane[j][:], in_=x4[:, j, :])
+            if j == PLANE_ORDER[0]:
                 nc.sync.dma_start(out=offs_t[:], in_=offs)
         for u, (a, b) in enumerate(w1_parts):
             nc.sync.dma_start(out=w1r[u][:], in_=w14[:, :, a:b])
@@ -94,8 +92,6 @@ def tile_picked_sub_mlp_relu_sub_e_kernel(tc, xT, w1, w2, gate, offs, pos1, pos2
         nc.sync.dma_start(out=pos_t[0][:], in_=pos1)
         nc.sync.dma_start(out=pos_t[1][:], in_=pos2)
         nc.sync.dma_start(out=gt[:], in_=gate[:, 0:P, :].rearrange("d p v -> p d v"))
-
-        nc.vector.memset(all_s[:].bitcast(I32), 0)
 
         def copy(engine, dst, src):
             if engine == "scalar":
@@ -118,12 +114,13 @@ def tile_picked_sub_mlp_relu_sub_e_kernel(tc, xT, w1, w2, gate, offs, pos1, pos2
         def quant(words, scales, woven):
             nc.vector.quantize_mx(out=words.bitcast(FP8X4), scales=scales, in_=woven)
 
-        def quant_slab(i):
-            a, b = slabs[i]
-            flat = x_bf[i][:].rearrange("p n j -> p (n j)")
-            cuts = (0, b - a) if b - a in (128, 256, 512) else (0, P, b - a)
-            for lo, hi in zip(cuts[:-1], cuts[1:]):
-                quant(all_c[:, a + lo : a + hi], all_s[:, a + lo : a + hi], flat[:, 4 * lo : 4 * hi])
+        def weave_x(q):
+            a, b = picks[q]
+            dst = xg[q][:].rearrange("p n (u e) -> p n u e", u=2)
+            nc.vector.tensor_copy(dst, pairs[:, :, a:b, :].rearrange("p u n e -> p n u e"))
+
+        def quant_x(q):
+            quant(xc[q][:], xs[q][:], xg[q][:].rearrange("p n j -> p (n j)"))
 
         def quant_w1(t0, t1):
             flat = w1g[:].rearrange("p t m j -> p (t m j)")
@@ -135,25 +132,23 @@ def tile_picked_sub_mlp_relu_sub_e_kernel(tc, xT, w1, w2, gate, offs, pos1, pos2
         def entries(list_tile, a, b):
             return list_tile[:, a // LIST_ROWS : b // LIST_ROWS]
 
-        def gather_words(q):
-            nc.vector.tensor_copy(xc[q][:], all_c[:].indirect(entries(offs_t, q * QUARTER, (q + 1) * QUARTER)))
-
-        def gather_bytes(q):
-            nc.vector.tensor_copy(xs[q][:], all_s[:].indirect(entries(offs_t, q * QUARTER, (q + 1) * QUARTER)))
+        def gather_plane(j, a, b):
+            nc.vector.tensor_copy(pairs[:, j // 2, a:b, j % 2], plane[j][:].indirect(entries(offs_t, a, b)))
 
         h_bank = {}
         y_bank = {}
 
         def layer1(c):
             h_bank[c] = take_bank(c)
-            cols = slice((c % 2) * P, (c % 2 + 1) * P)
+            q = max(i for i, (a, b) in enumerate(picks) if a <= c * P)
+            cols = slice(c * P - picks[q][0], (c + 1) * P - picks[q][0])
             for t in range(4):
                 nc.tensor.matmul_mx(
                     out=h_bank[c][:, t, :],
                     lhsT=w1c[:, t * P : (t + 1) * P].bitcast(FP8X4),
                     lhsT_scale=w1s[:, t * P : (t + 1) * P],
-                    rhs=xc[c // 2][:, cols].bitcast(FP8X4),
-                    rhs_scale=xs[c // 2][:, cols],
+                    rhs=xc[q][:, cols].bitcast(FP8X4),
+                    rhs_scale=xs[q][:, cols],
                     start=True,
                     stop=True,
                 )
@@ -189,46 +184,47 @@ def tile_picked_sub_mlp_relu_sub_e_kernel(tc, xT, w1, w2, gate, offs, pos1, pos2
             nc.vector.tensor_tensor(res[m][:, a:b], part[m][0][:, a:b], part[m][1][:, a:b], ADD)
             nc.sync.dma_start(out=out[m * P : (m + 1) * P, a:b], in_=res[m][:, a:b])
 
-        for i, (a, b) in enumerate(slabs):
-            n = b - a
-            weave("scalar", x_bf[i], x_raw[i], 0, SCALAR_SHARE[i])
-            weave("vector", x_bf[i], x_raw[i], SCALAR_SHARE[i], n)
-            if i > 0:
-                quant_slab(i - 1)
-        quant_slab(len(slabs) - 1)
-
+        nc.scalar.copy(plane_bf[0][:], plane[0][:])
+        nc.scalar.copy(plane_bf[1][:, 0 : T // 2], plane[1][:, 0 : T // 2])
+        nc.gpsimd.tensor_copy(plane_bf[1][:, T // 2 : T], plane[1][:, T // 2 : T])
+        for j in PLANE_ORDER[:-1]:
+            gather_plane(j, 0, S - SCALAR_ENTRIES if j < 2 else S)
+        for j in range(2):
+            looked_up = plane_bf[j][:].indirect(entries(offs_t, S - SCALAR_ENTRIES, S))
+            nc.scalar.activation(pairs[:, 0, S - SCALAR_ENTRIES : S, j], looked_up, COPY)
+        gather_plane(PLANE_ORDER[-1], 0, 256)
+        gather_plane(PLANE_ORDER[-1], 256, S)
         for u in range(len(w1_parts)):
             weave_w1(u)
-        for q in (0, 1):
-            gather_words(q)
-            gather_bytes(q)
+        weave_x(0)
+        weave_x(1)
+        quant_x(0)
         quant_w1(0, 2)
-        quant_w1(2, 4)
+        quant_w1(2, 3)
+        quant_w1(3, 4)
         weave("scalar", w2g, w2r, 0, N)
 
-        for c in range(4):
+        weave_x(2)
+        quant_x(1)
+        quant_x(2)
+        for c in range(8):
             layer1(c)
-        for q in (2, 3):
-            gather_words(q)
-            gather_bytes(q)
-        for c in range(4, 8):
-            layer1(c)
-        for c in (0, 1, 2, 3, 5, 6):
+        for c in (0, 1, 2, 3, 6, 7):
             relu_out("scalar", c)
         quant(w2c[:], w2s[:], w2g[:].rearrange("p n j -> p (n j)"))
 
         relu_out("vector", 4)
+        relu_out("vector", 5)
         quant_h(0, 512)
         layer2(0, 0, 512, 0)
         quant_h(512, 768)
-        layer2(0, 512, 768, 1)
-        relu_out("vector", 7)
         quant_h(768, 896)
         layer2(0, 768, 896, 2)
         quant_h(896, 1024)
         layer2(0, 896, 1024, 3)
+        layer2(0, 512, 768, 7)
         y_out("scalar", 0, 0, 512)
-        y_out("scalar", 0, 512, 768)
+        y_out("vector", 0, 512, 768)
         y_out("scalar", 0, 768, 896)
         y_out("scalar", 0, 896, 1024)
         layer2(1, 0, 512, 2)

@@ -24,6 +24,7 @@ FLOPS = 2 * S * H * K + 2 * S * N * H
 PLANE_ORDER = (0, 2, 1, 3)
 SCALAR_ENTRIES = 256
 LIST_CUTS = (0, 256, 512, 1024)
+WARM_UPS = 5
 W1_CUTS = (0, 160, 352, 512)
 LIST_ROWS = 16
 
@@ -52,16 +53,18 @@ def tile_picked_sub_mlp_relu_sub_e_kernel(tc, xT, w1, w2, gate, offs, pos1, pos2
 
         offs_t = keep.tile([P, S // LIST_ROWS], U16, name="offs_t")
         pos_t = [keep.tile([P, V // LIST_ROWS], U16, name=f"pos_t{d}") for d in range(2)]
-        plane = [own(f"plane{j}", [P, T], F32) for j in range(4)]
+        spare = 4 * (W1_CUTS[2] - W1_CUTS[1])
+        plane = [own(f"plane{j}", [P, T + (spare if j == PLANE_ORDER[-1] else 0)], F32) for j in range(4)]
         plane_bf = [own(f"plane_bf{j}", [P, T], BF16) for j in range(2)]
         pairs = own("pairs", [P, 2, S, 2], BF16)
         w1g = placed("w1g", [P, 4, P, 4], BF16, AT_W1)
         picks = list(zip(LIST_CUTS[:-1], LIST_CUTS[1:]))
-        xg = [own("xg0", [P, 256, 4], BF16), own("xg1", [P, 256, 4], BF16), placed("xg2", [P, 512, 4], BF16, AT_XG2)]
+        xg = [own("xg0", [P, 256, 4], BF16)[:], own("xg1", [P, 256, 4], BF16)[:], placed("xg2", [P, 512, 4], BF16, AT_XG2)[:]]
         xc = [own("xc0", [P, 256], U32), placed("xc1", [P, 256], U32, AT_XC1), own("xc2", [P, 512], U32)]
         xs = [own(f"xs{q}", [P, b - a], U8) for q, (a, b) in enumerate(picks)]
         w1_parts = list(zip(W1_CUTS[:-1], W1_CUTS[1:]))
-        w1r = [own(f"w1r{u}", [P, 4, b - a], F32) for u, (a, b) in enumerate(w1_parts)]
+        w1r = {u: own(f"w1r{u}", [P, 4, b - a], F32)[:] for u, (a, b) in enumerate(w1_parts) if u != 1}
+        w1r[1] = plane[PLANE_ORDER[-1]][:, T : T + spare].rearrange("p (j c) -> p j c", j=4)
         w1c = own("w1c", [P, H], U32)
         w1s = own("w1s", [P, H], U8)
         w2r = placed("w2r", [P, 4, N], F32, AT_W2)
@@ -83,11 +86,11 @@ def tile_picked_sub_mlp_relu_sub_e_kernel(tc, xT, w1, w2, gate, offs, pos1, pos2
         x4 = xT.rearrange("(p j) t -> p j t", j=4)
         w14 = w1.rearrange("(p j) c -> p j c", j=4)
         for j in PLANE_ORDER:
-            nc.sync.dma_start(out=plane[j][:], in_=x4[:, j, :])
+            nc.sync.dma_start(out=plane[j][:, 0:T], in_=x4[:, j, :])
             if j == PLANE_ORDER[0]:
                 nc.sync.dma_start(out=offs_t[:], in_=offs)
         for u, (a, b) in enumerate(w1_parts):
-            nc.sync.dma_start(out=w1r[u][:], in_=w14[:, :, a:b])
+            nc.sync.dma_start(out=w1r[u], in_=w14[:, :, a:b])
         nc.sync.dma_start(out=w2r[:], in_=w2.rearrange("(p j) n -> p j n", j=4))
         nc.sync.dma_start(out=pos_t[0][:], in_=pos1)
         nc.sync.dma_start(out=pos_t[1][:], in_=pos2)
@@ -109,18 +112,18 @@ def tile_picked_sub_mlp_relu_sub_e_kernel(tc, xT, w1, w2, gate, offs, pos1, pos2
         def weave_w1(u):
             a, b = w1_parts[u]
             dst = w1g[:, :, a // 4 : b // 4, :].rearrange("p t m j -> p m j t")
-            nc.scalar.copy(dst, w1r[u][:].rearrange("p j (m t) -> p m j t", t=4))
+            nc.scalar.copy(dst, w1r[u].rearrange("p j (m t) -> p m j t", t=4))
 
         def quant(words, scales, woven):
             nc.vector.quantize_mx(out=words.bitcast(FP8X4), scales=scales, in_=woven)
 
         def weave_x(q):
             a, b = picks[q]
-            dst = xg[q][:].rearrange("p n (u e) -> p n u e", u=2)
+            dst = xg[q].rearrange("p n (u e) -> p n u e", u=2)
             nc.vector.tensor_copy(dst, pairs[:, :, a:b, :].rearrange("p u n e -> p n u e"))
 
         def quant_x(q):
-            quant(xc[q][:], xs[q][:], xg[q][:].rearrange("p n j -> p (n j)"))
+            quant(xc[q][:], xs[q][:], xg[q].rearrange("p n j -> p (n j)"))
 
         def quant_w1(t0, t1):
             flat = w1g[:].rearrange("p t m j -> p (t m j)")
@@ -132,8 +135,8 @@ def tile_picked_sub_mlp_relu_sub_e_kernel(tc, xT, w1, w2, gate, offs, pos1, pos2
         def entries(list_tile, a, b):
             return list_tile[:, a // LIST_ROWS : b // LIST_ROWS]
 
-        def gather_plane(j, a, b):
-            nc.vector.tensor_copy(pairs[:, j // 2, a:b, j % 2], plane[j][:].indirect(entries(offs_t, a, b)))
+        def gather_plane(j, a, b, width=T):
+            nc.vector.tensor_copy(pairs[:, j // 2, a:b, j % 2], plane[j][:, 0:width].indirect(entries(offs_t, a, b)))
 
         h_bank = {}
         y_bank = {}
@@ -193,12 +196,24 @@ def tile_picked_sub_mlp_relu_sub_e_kernel(tc, xT, w1, w2, gate, offs, pos1, pos2
             looked_up = plane_bf[j][:].indirect(entries(offs_t, S - SCALAR_ENTRIES, S))
             nc.scalar.activation(pairs[:, 0, S - SCALAR_ENTRIES : S, j], looked_up, COPY)
         gather_plane(PLANE_ORDER[-1], 0, 256)
-        gather_plane(PLANE_ORDER[-1], 256, S)
-        for u in range(len(w1_parts)):
-            weave_w1(u)
+        gather_plane(PLANE_ORDER[-1], 256, 512)
         weave_x(0)
         weave_x(1)
         quant_x(0)
+        warm = take_bank(7)[:].rearrange("p t n -> p (t n)")[:, 0:256]
+        for rep in range(WARM_UPS):
+            nc.tensor.matmul_mx(
+                out=warm,
+                lhsT=xc[0][:, 0:P].bitcast(FP8X4),
+                lhsT_scale=xs[0][:, 0:P],
+                rhs=xc[0][:].bitcast(FP8X4),
+                rhs_scale=xs[0][:],
+                start=True,
+                stop=True,
+            )
+        gather_plane(PLANE_ORDER[-1], S // 2, S, T + 8)
+        for u in range(len(w1_parts)):
+            weave_w1(u)
         quant_w1(0, 2)
         quant_w1(2, 3)
         quant_w1(3, 4)

@@ -25,14 +25,19 @@ PLANE_ORDER = (0, 2, 1, 3)
 SCALAR_ENTRIES = 256
 LIST_CUTS = (0, 256, 512, 1024)
 WARM_UPS = 5
-W1_CUTS = (0, 160, 352, 512)
+CHUNKS = (
+    (0, 128, 0), (128, 256, 1), (256, 384, 2), (384, 512, 3), (512, 640, 4),
+    (640, 704, 5), (704, 768, 0), (768, 896, 6), (896, 1024, 7),
+)
+W1_CUTS = (0, 256, 512)
+GPSIMD_W1 = (0, 80)
 LIST_ROWS = 16
 
 AT_W1 = 0
 AT_XC1 = AT_W1
 AT_XG2 = AT_W1 + 1024
 AT_W2 = 5120
-H_PIECES = ((512, AT_W2 + 3072), (256, AT_W2), (P, AT_W2 + 2048), (P, AT_W2 + 7168))
+H_PIECES = ((512, AT_W2 + 3584), (256, AT_W2 + 512), (P, AT_W2 + 2560), (P, AT_W2 + 7680))
 
 
 def tile_picked_sub_mlp_relu_sub_e_kernel(tc, xT, w1, w2, gate, offs, pos1, pos2, out):
@@ -53,7 +58,7 @@ def tile_picked_sub_mlp_relu_sub_e_kernel(tc, xT, w1, w2, gate, offs, pos1, pos2
 
         offs_t = keep.tile([P, S // LIST_ROWS], U16, name="offs_t")
         pos_t = [keep.tile([P, V // LIST_ROWS], U16, name=f"pos_t{d}") for d in range(2)]
-        spare = 4 * (W1_CUTS[2] - W1_CUTS[1])
+        spare = 4 * W1_CUTS[1]
         plane = [own(f"plane{j}", [P, T + (spare if j == PLANE_ORDER[-1] else 0)], F32) for j in range(4)]
         plane_bf = [own(f"plane_bf{j}", [P, T], BF16) for j in range(2)]
         pairs = own("pairs", [P, 2, S, 2], BF16)
@@ -63,11 +68,11 @@ def tile_picked_sub_mlp_relu_sub_e_kernel(tc, xT, w1, w2, gate, offs, pos1, pos2
         xc = [own("xc0", [P, 256], U32), placed("xc1", [P, 256], U32, AT_XC1), own("xc2", [P, 512], U32)]
         xs = [own(f"xs{q}", [P, b - a], U8) for q, (a, b) in enumerate(picks)]
         w1_parts = list(zip(W1_CUTS[:-1], W1_CUTS[1:]))
-        w1r = {u: own(f"w1r{u}", [P, 4, b - a], F32)[:] for u, (a, b) in enumerate(w1_parts) if u != 1}
-        w1r[1] = plane[PLANE_ORDER[-1]][:, T : T + spare].rearrange("p (j c) -> p j c", j=4)
+        w1r = {u: own(f"w1r{u}", [P, 4, b - a], F32)[:] for u, (a, b) in enumerate(w1_parts) if u != 0}
+        w1r[0] = plane[PLANE_ORDER[-1]][:, T : T + spare].rearrange("p (j c) -> p j c", j=4)
         w1c = own("w1c", [P, H], U32)
         w1s = own("w1s", [P, H], U8)
-        w2r = placed("w2r", [P, 4, N], F32, AT_W2)
+        w2r = [placed(f"w2r{m}", [P, 4, P], F32, AT_W2 + 2048 * m) for m in range(2)]
         w2g = own("w2g", [P, N, 4], BF16)
         w2c = own("w2c", [P, N], U32)
         w2s = own("w2s", [P, N], U8)
@@ -91,7 +96,8 @@ def tile_picked_sub_mlp_relu_sub_e_kernel(tc, xT, w1, w2, gate, offs, pos1, pos2
                 nc.sync.dma_start(out=offs_t[:], in_=offs)
         for u, (a, b) in enumerate(w1_parts):
             nc.sync.dma_start(out=w1r[u], in_=w14[:, :, a:b])
-        nc.sync.dma_start(out=w2r[:], in_=w2.rearrange("(p j) n -> p j n", j=4))
+        for m in range(2):
+            nc.sync.dma_start(out=w2r[m][:], in_=w2.rearrange("(p j) n -> p j n", j=4)[:, :, m * P : (m + 1) * P])
         nc.sync.dma_start(out=pos_t[0][:], in_=pos1)
         nc.sync.dma_start(out=pos_t[1][:], in_=pos2)
         nc.sync.dma_start(out=gt[:], in_=gate[:, 0:P, :].rearrange("d p v -> p d v"))
@@ -111,8 +117,12 @@ def tile_picked_sub_mlp_relu_sub_e_kernel(tc, xT, w1, w2, gate, offs, pos1, pos2
 
         def weave_w1(u):
             a, b = w1_parts[u]
-            dst = w1g[:, :, a // 4 : b // 4, :].rearrange("p t m j -> p m j t")
-            nc.scalar.copy(dst, w1r[u].rearrange("p j (m t) -> p m j t", t=4))
+            cut = b - a - GPSIMD_W1[u]
+            dst = w1g[:, :, a // 4 : (a + cut) // 4, :].rearrange("p t m j -> p m j t")
+            nc.scalar.copy(dst, w1r[u][:, :, 0:cut].rearrange("p j (m t) -> p m j t", t=4))
+            if GPSIMD_W1[u]:
+                src = w1r[u][:, :, cut : b - a].rearrange("p j (m t) -> p t m j", t=4)
+                nc.gpsimd.tensor_scalar(w1g[:, :, (a + cut) // 4 : b // 4, :], src, 1.0, 0.0, MULT, ADD)
 
         def quant(words, scales, woven):
             nc.vector.quantize_mx(out=words.bitcast(FP8X4), scales=scales, in_=woven)
@@ -141,13 +151,13 @@ def tile_picked_sub_mlp_relu_sub_e_kernel(tc, xT, w1, w2, gate, offs, pos1, pos2
         h_bank = {}
         y_bank = {}
 
-        def layer1(c):
-            h_bank[c] = take_bank(c)
-            q = max(i for i, (a, b) in enumerate(picks) if a <= c * P)
-            cols = slice(c * P - picks[q][0], (c + 1) * P - picks[q][0])
+        def layer1(a, b, bank):
+            h_bank[a] = take_bank(bank)[:, :, 0 : b - a]
+            q = max(i for i, (lo, hi) in enumerate(picks) if lo <= a)
+            cols = slice(a - picks[q][0], b - picks[q][0])
             for t in range(4):
                 nc.tensor.matmul_mx(
-                    out=h_bank[c][:, t, :],
+                    out=h_bank[a][:, t, :],
                     lhsT=w1c[:, t * P : (t + 1) * P].bitcast(FP8X4),
                     lhsT_scale=w1s[:, t * P : (t + 1) * P],
                     rhs=xc[q][:, cols].bitcast(FP8X4),
@@ -156,10 +166,11 @@ def tile_picked_sub_mlp_relu_sub_e_kernel(tc, xT, w1, w2, gate, offs, pos1, pos2
                     stop=True,
                 )
 
-        def relu_out(engine, c):
-            piece, nth = h_place[c]
-            dst = hg[piece][:, nth * P : (nth + 1) * P, :]
-            src = h_bank[c][:].rearrange("p t n -> p n t")
+        def relu_out(engine, a, b):
+            piece, nth = h_place[a // P]
+            first = nth * P + a % P
+            dst = hg[piece][:, first : first + b - a, :]
+            src = h_bank[a].rearrange("p t n -> p n t")
             if engine == "scalar":
                 nc.scalar.activation(dst, src, RELU)
             else:
@@ -217,21 +228,25 @@ def tile_picked_sub_mlp_relu_sub_e_kernel(tc, xT, w1, w2, gate, offs, pos1, pos2
         quant_w1(0, 2)
         quant_w1(2, 3)
         quant_w1(3, 4)
-        weave("scalar", w2g, w2r, 0, N)
+        for m in range(2):
+            weave("scalar", w2g[:, m * P : (m + 1) * P, :], w2r[m], 0, P)
 
         weave_x(2)
         quant_x(1)
         quant_x(2)
-        for c in range(8):
-            layer1(c)
-        for c in (0, 1, 2, 3, 6, 7):
-            relu_out("scalar", c)
+        for a, b, bank in CHUNKS[:6]:
+            layer1(a, b, bank)
+        relu_out("scalar", *CHUNKS[0][:2])
+        for a, b, bank in CHUNKS[6:]:
+            layer1(a, b, bank)
+        for c in (1, 2, 3, 6, 7, 8):
+            relu_out("scalar", *CHUNKS[c][:2])
         quant(w2c[:], w2s[:], w2g[:].rearrange("p n j -> p (n j)"))
 
-        relu_out("vector", 4)
-        relu_out("vector", 5)
+        relu_out("vector", *CHUNKS[4][:2])
+        relu_out("vector", *CHUNKS[5][:2])
         quant_h(0, 512)
-        layer2(0, 0, 512, 0)
+        layer2(0, 0, 512, 1)
         quant_h(512, 768)
         quant_h(768, 896)
         layer2(0, 768, 896, 2)
@@ -267,8 +282,9 @@ def tile_picked_sub_mlp_relu_sub_e_kernel(tc, xT, w1, w2, gate, offs, pos1, pos2
             nc.scalar.copy(turned_sum[:, k, :], turned[k][:, 0, :])
             nc.tensor.transpose(back[k // 2][:, k % 2, :], turned_sum[:, k, :], ident[:])
         for u in range(2):
-            nc.scalar.copy(res[0][:, 2 * u * P : 2 * (u + 1) * P], back[u][:, 0:2, :].rearrange("p t n -> p (t n)"))
-        nc.scalar.dma_start(out=out[0:P, :], in_=res[0][:])
+            cols = slice(2 * u * P, 2 * (u + 1) * P)
+            nc.scalar.copy(res[0][:, cols], back[u][:, 0:2, :].rearrange("p t n -> p (t n)"))
+            nc.scalar.dma_start(out=out[0:P, cols], in_=res[0][:, cols])
         fetch(1, 1, 0, V // 2)
         fetch(1, 1, V // 2, V)
         finish(1, 0, V // 2)

@@ -27,7 +27,7 @@ LIST_CUTS = (0, 256, 512, 1024)
 WARM_UPS = 5
 CHUNKS = (
     (0, 128, 0), (128, 256, 1), (256, 384, 2), (384, 512, 3), (512, 640, 4),
-    (640, 704, 5), (704, 768, 0), (768, 896, 6), (896, 1024, 7),
+    (640, 768, 5), (768, 896, 6), (896, 1024, 7),
 )
 W1_CUTS = (0, 256, 512)
 GPSIMD_W1 = (0, 80)
@@ -239,11 +239,11 @@ def tile_picked_sub_mlp_relu_sub_e_kernel(tc, xT, w1, w2, gate, offs, pos1, pos2
         relu_out("scalar", *CHUNKS[0][:2])
         for a, b, bank in CHUNKS[6:]:
             layer1(a, b, bank)
-        for c in (1, 2, 3, 6, 7, 8):
+        for c in (1, 3, 4, 6, 7):
             relu_out("scalar", *CHUNKS[c][:2])
         quant(w2c[:], w2s[:], w2g[:].rearrange("p n j -> p (n j)"))
 
-        relu_out("vector", *CHUNKS[4][:2])
+        relu_out("vector", *CHUNKS[2][:2])
         relu_out("vector", *CHUNKS[5][:2])
         quant_h(0, 512)
         layer2(0, 0, 512, 1)

@@ -1,7 +1,6 @@
 from contextlib import ExitStack
 
 import concourse.mybir as mybir
-from concourse.masks import make_identity
 
 K, T, S, H, N, V = 512, 2048, 1024, 512, 256, 512
 P = 128
@@ -20,24 +19,23 @@ ADD = mybir.AluOpType.add
 MAX = mybir.AluOpType.max
 
 FLOPS = 2 * S * H * K + 2 * S * N * H
+LIST_ROWS = 16
 
 PLANE_ORDER = (0, 2, 1, 3)
 SCALAR_ENTRIES = 256
 LIST_CUTS = (0, 256, 512, 1024)
-WARM_UPS = 5
-CHUNKS = (
-    (0, 128, 0), (128, 256, 1), (256, 384, 2), (384, 512, 3), (512, 640, 4),
-    (640, 768, 5), (768, 896, 6), (896, 1024, 7),
-)
-W1_CUTS = (0, 256, 512)
-GPSIMD_W1 = (0, 80)
-LIST_ROWS = 16
+W1_SCALAR = ((0, 128), (416, 512))
+W1_VECTOR = ((128, 256), (256, 416))
+VECTOR_CHUNKS = (3, 6)
 
-AT_W1 = 0
-AT_XC1 = AT_W1
-AT_XG2 = AT_W1 + 1024
-AT_W2 = 5120
-H_PIECES = ((512, AT_W2 + 3584), (256, AT_W2 + 512), (P, AT_W2 + 2560), (P, AT_W2 + 7680))
+AT_W1G = 0
+AT_XC1 = AT_W1G
+AT_XC2 = AT_W1G + 1024
+AT_W1B = 4096
+AT_XC0 = AT_W1B
+AT_XG2 = AT_W1B + 1024
+AT_W2G1 = AT_XG2
+H_PIECES = (512, 256, P, P)
 
 
 def tile_picked_sub_mlp_relu_sub_e_kernel(tc, xT, w1, w2, gate, offs, pos1, pos2, out):
@@ -58,44 +56,39 @@ def tile_picked_sub_mlp_relu_sub_e_kernel(tc, xT, w1, w2, gate, offs, pos1, pos2
 
         offs_t = keep.tile([P, S // LIST_ROWS], U16, name="offs_t")
         pos_t = [keep.tile([P, V // LIST_ROWS], U16, name=f"pos_t{d}") for d in range(2)]
-        spare = 4 * W1_CUTS[1]
-        plane = [own(f"plane{j}", [P, T + (spare if j == PLANE_ORDER[-1] else 0)], F32) for j in range(4)]
-        plane_bf = [own(f"plane_bf{j}", [P, T], BF16) for j in range(2)]
+        plane = [own(f"plane{j}", [P, T], F32) for j in range(4)]
+        side = own("side", [P, 4, SCALAR_ENTRIES], BF16)
         pairs = own("pairs", [P, 2, S, 2], BF16)
-        w1g = placed("w1g", [P, 4, P, 4], BF16, AT_W1)
+        w1g = placed("w1g", [P, 4, P, 4], BF16, AT_W1G)
         picks = list(zip(LIST_CUTS[:-1], LIST_CUTS[1:]))
-        xg = [own("xg0", [P, 256, 4], BF16)[:], own("xg1", [P, 256, 4], BF16)[:], placed("xg2", [P, 512, 4], BF16, AT_XG2)[:]]
-        xc = [own("xc0", [P, 256], U32), placed("xc1", [P, 256], U32, AT_XC1), own("xc2", [P, 512], U32)]
+        xg = [own("xg0", [P, 256, 4], BF16), own("xg1", [P, 256, 4], BF16), placed("xg2", [P, 512, 4], BF16, AT_XG2)]
+        xc = [placed("xc0", [P, 256], U32, AT_XC0), placed("xc1", [P, 256], U32, AT_XC1), placed("xc2", [P, 512], U32, AT_XC2)]
         xs = [own(f"xs{q}", [P, b - a], U8) for q, (a, b) in enumerate(picks)]
-        w1_parts = list(zip(W1_CUTS[:-1], W1_CUTS[1:]))
-        w1r = {u: own(f"w1r{u}", [P, 4, b - a], F32)[:] for u, (a, b) in enumerate(w1_parts) if u != 0}
-        w1r[0] = plane[PLANE_ORDER[-1]][:, T : T + spare].rearrange("p (j c) -> p j c", j=4)
+        w1r = [own("w1r0", [P, 4, 256], F32), placed("w1r1", [P, 4, 256], F32, AT_W1B)]
         w1c = own("w1c", [P, H], U32)
         w1s = own("w1s", [P, H], U8)
-        w2r = [placed(f"w2r{m}", [P, 4, P], F32, AT_W2 + 2048 * m) for m in range(2)]
-        w2g = own("w2g", [P, N, 4], BF16)
+        w2r = [own(f"w2r{m}", [P, 4, P], F32) for m in range(2)]
+        w2g = [own("w2g0", [P, P, 4], BF16), placed("w2g1", [P, P, 4], BF16, AT_W2G1)]
         w2c = own("w2c", [P, N], U32)
         w2s = own("w2s", [P, N], U8)
-        hg = [placed(f"hg{i}", [P, n, 4], BF16, at) for i, (n, at) in enumerate(H_PIECES)]
-        h_place = [(i, nth) for i, (n, at) in enumerate(H_PIECES) for nth in range(n // P)]
+        hg = [own(f"hg{i}", [P, n, 4], BF16) for i, n in enumerate(H_PIECES)]
+        h_place = [(i, nth) for i, n in enumerate(H_PIECES) for nth in range(n // P)]
         hc = own("hc", [P, S], U32)
         hs = own("hs", [P, S], U8)
         y = [own(f"y{m}", [P, S], F32) for m in range(2)]
         gt = own("gt", [P, 2, V], F32)
+        plain = [own(f"plain{m}", [P, V], F32) for m in range(2)]
         part = [[own(f"part{m}{d}", [P, V], F32) for d in range(2)] for m in range(2)]
         res = [own(f"res{m}", [P, V], F32) for m in range(2)]
-        ident = own("ident", [P, P], F32)
-        turned_sum = own("turned_sum", [P, 4, P], F32)
-        make_identity(nc, ident[:])
 
         x4 = xT.rearrange("(p j) t -> p j t", j=4)
         w14 = w1.rearrange("(p j) c -> p j c", j=4)
         for j in PLANE_ORDER:
-            nc.sync.dma_start(out=plane[j][:, 0:T], in_=x4[:, j, :])
+            nc.sync.dma_start(out=plane[j][:], in_=x4[:, j, :])
             if j == PLANE_ORDER[0]:
                 nc.sync.dma_start(out=offs_t[:], in_=offs)
-        for u, (a, b) in enumerate(w1_parts):
-            nc.sync.dma_start(out=w1r[u], in_=w14[:, :, a:b])
+        for u in range(2):
+            nc.sync.dma_start(out=w1r[u][:], in_=w14[:, :, 256 * u : 256 * (u + 1)])
         for m in range(2):
             nc.sync.dma_start(out=w2r[m][:], in_=w2.rearrange("(p j) n -> p j n", j=4)[:, :, m * P : (m + 1) * P])
         nc.sync.dma_start(out=pos_t[0][:], in_=pos1)
@@ -108,36 +101,36 @@ def tile_picked_sub_mlp_relu_sub_e_kernel(tc, xT, w1, w2, gate, offs, pos1, pos2
             else:
                 nc.vector.tensor_copy(dst, src)
 
-        def weave(engine, dst, src, a, b):
-            copy(
-                engine,
-                dst[:, a:b, :].rearrange("p (c i) j -> p c j i", i=4),
-                src[:, :, a:b].rearrange("p j (c i) -> p c j i", i=4),
-            )
+        def weave_w1(engine, a, b):
+            u = a // 256
+            src = w1r[u][:, :, a - 256 * u : b - 256 * u]
+            dst = w1g[:, :, a // 4 : b // 4, :]
+            if engine == "gpsimd":
+                nc.gpsimd.tensor_scalar(dst, src.rearrange("p j (m t) -> p t m j", t=4), 1.0, 0.0, MULT, ADD)
+            else:
+                copy(engine, dst.rearrange("p t m j -> p m j t"), src.rearrange("p j (m t) -> p m j t", t=4))
 
-        def weave_w1(u):
-            a, b = w1_parts[u]
-            cut = b - a - GPSIMD_W1[u]
-            dst = w1g[:, :, a // 4 : (a + cut) // 4, :].rearrange("p t m j -> p m j t")
-            nc.scalar.copy(dst, w1r[u][:, :, 0:cut].rearrange("p j (m t) -> p m j t", t=4))
-            if GPSIMD_W1[u]:
-                src = w1r[u][:, :, cut : b - a].rearrange("p j (m t) -> p t m j", t=4)
-                nc.gpsimd.tensor_scalar(w1g[:, :, (a + cut) // 4 : b // 4, :], src, 1.0, 0.0, MULT, ADD)
+        def weave(engine, dst, src):
+            copy(engine, dst.rearrange("p (c i) j -> p c j i", i=4), src.rearrange("p j (c i) -> p c j i", i=4))
 
         def quant(words, scales, woven):
             nc.vector.quantize_mx(out=words.bitcast(FP8X4), scales=scales, in_=woven)
 
-        def weave_x(q):
+        def weave_x(engine, q):
             a, b = picks[q]
-            dst = xg[q].rearrange("p n (u e) -> p n u e", u=2)
-            nc.vector.tensor_copy(dst, pairs[:, :, a:b, :].rearrange("p u n e -> p n u e"))
+            dst = xg[q][:].rearrange("p n j -> p (n j)").bitcast(U32).rearrange("p (n u) -> p n u", u=2)
+            words = pairs[:].rearrange("p u n e -> p u (n e)").bitcast(U32)
+            copy(engine, dst, words[:, :, a:b].rearrange("p u n -> p n u"))
 
         def quant_x(q):
-            quant(xc[q][:], xs[q][:], xg[q].rearrange("p n j -> p (n j)"))
+            quant(xc[q][:], xs[q][:], xg[q][:].rearrange("p n j -> p (n j)"))
 
         def quant_w1(t0, t1):
             flat = w1g[:].rearrange("p t m j -> p (t m j)")
             quant(w1c[:, t0 * P : t1 * P], w1s[:, t0 * P : t1 * P], flat[:, 4 * t0 * P : 4 * t1 * P])
+
+        def quant_w2(m):
+            quant(w2c[:, m * P : (m + 1) * P], w2s[:, m * P : (m + 1) * P], w2g[m][:].rearrange("p n j -> p (n j)"))
 
         def quant_h(a, b):
             quant(hc[:, a:b], hs[:, a:b], hg[h_place[a // P][0]][:].rearrange("p n j -> p (n j)"))
@@ -145,19 +138,20 @@ def tile_picked_sub_mlp_relu_sub_e_kernel(tc, xT, w1, w2, gate, offs, pos1, pos2
         def entries(list_tile, a, b):
             return list_tile[:, a // LIST_ROWS : b // LIST_ROWS]
 
-        def gather_plane(j, a, b, width=T):
-            nc.vector.tensor_copy(pairs[:, j // 2, a:b, j % 2], plane[j][:, 0:width].indirect(entries(offs_t, a, b)))
+        def gather_plane(j, a, b):
+            nc.vector.tensor_copy(pairs[:, j // 2, a:b, j % 2], plane[j][:].indirect(entries(offs_t, a, b)))
 
         h_bank = {}
         y_bank = {}
 
-        def layer1(a, b, bank):
-            h_bank[a] = take_bank(bank)[:, :, 0 : b - a]
+        def layer1(c):
+            a, b = c * P, (c + 1) * P
+            h_bank[c] = take_bank(c)
             q = max(i for i, (lo, hi) in enumerate(picks) if lo <= a)
             cols = slice(a - picks[q][0], b - picks[q][0])
             for t in range(4):
                 nc.tensor.matmul_mx(
-                    out=h_bank[a][:, t, :],
+                    out=h_bank[c][:, t, :],
                     lhsT=w1c[:, t * P : (t + 1) * P].bitcast(FP8X4),
                     lhsT_scale=w1s[:, t * P : (t + 1) * P],
                     rhs=xc[q][:, cols].bitcast(FP8X4),
@@ -166,20 +160,21 @@ def tile_picked_sub_mlp_relu_sub_e_kernel(tc, xT, w1, w2, gate, offs, pos1, pos2
                     stop=True,
                 )
 
-        def relu_out(engine, a, b):
-            piece, nth = h_place[a // P]
-            first = nth * P + a % P
-            dst = hg[piece][:, first : first + b - a, :]
-            src = h_bank[a].rearrange("p t n -> p n t")
-            if engine == "scalar":
-                nc.scalar.activation(dst, src, RELU)
-            else:
+        def relu_out(c):
+            piece, nth = h_place[c]
+            dst = hg[piece][:, nth * P : (nth + 1) * P, :]
+            src = h_bank[c][:].rearrange("p t n -> p n t")
+            if c in VECTOR_CHUNKS:
                 nc.vector.tensor_scalar(dst, src, 0.0, None, MAX)
+            else:
+                nc.scalar.activation(dst, src, RELU)
 
-        def layer2(m, a, b, bank):
-            y_bank[m, a] = take_bank(bank)[:].rearrange("p t n -> p (t n)")[:, 0 : b - a]
+        def y_bank_for(m, a, bank):
+            y_bank[m, a] = take_bank(bank)[:].rearrange("p t n -> p (t n)")
+
+        def layer2(m, first, a, b):
             nc.tensor.matmul_mx(
-                out=y_bank[m, a],
+                out=y_bank[m, first][:, a - first : b - first],
                 lhsT=w2c[:, m * P : (m + 1) * P].bitcast(FP8X4),
                 lhsT_scale=w2s[:, m * P : (m + 1) * P],
                 rhs=hc[:, a:b].bitcast(FP8X4),
@@ -189,103 +184,79 @@ def tile_picked_sub_mlp_relu_sub_e_kernel(tc, xT, w1, w2, gate, offs, pos1, pos2
             )
 
         def y_out(engine, m, a, b):
-            copy(engine, y[m][:, a:b], y_bank[m, a])
+            copy(engine, y[m][:, a:b], y_bank[m, a][:, 0 : b - a])
 
-        def fetch(m, d, a, b):
-            nc.vector.tensor_tensor(part[m][d][:, a:b], y[m][:].indirect(entries(pos_t[d], a, b)), gt[:, d, a:b], MULT)
+        def fetch_gated(m, a, b):
+            nc.vector.tensor_tensor(part[m][0][:, a:b], y[m][:].indirect(entries(pos_t[0], a, b)), gt[:, 0, a:b], MULT)
+
+        def fetch_plain(m, a, b):
+            nc.scalar.activation(plain[m][:, a:b], y[m][:].indirect(entries(pos_t[1], a, b)), COPY)
+
+        def gate_plain(m, a, b):
+            nc.vector.tensor_tensor(part[m][1][:, a:b], plain[m][:, a:b], gt[:, 1, a:b], MULT)
 
         def finish(m, a, b):
             nc.vector.tensor_tensor(res[m][:, a:b], part[m][0][:, a:b], part[m][1][:, a:b], ADD)
             nc.sync.dma_start(out=out[m * P : (m + 1) * P, a:b], in_=res[m][:, a:b])
 
-        nc.scalar.copy(plane_bf[0][:], plane[0][:])
-        nc.scalar.copy(plane_bf[1][:, 0 : T // 2], plane[1][:, 0 : T // 2])
-        nc.gpsimd.tensor_copy(plane_bf[1][:, T // 2 : T], plane[1][:, T // 2 : T])
-        for j in PLANE_ORDER[:-1]:
-            gather_plane(j, 0, S - SCALAR_ENTRIES if j < 2 else S)
-        for j in range(2):
-            looked_up = plane_bf[j][:].indirect(entries(offs_t, S - SCALAR_ENTRIES, S))
-            nc.scalar.activation(pairs[:, 0, S - SCALAR_ENTRIES : S, j], looked_up, COPY)
-        gather_plane(PLANE_ORDER[-1], 0, 256)
-        gather_plane(PLANE_ORDER[-1], 256, 512)
-        weave_x(0)
-        weave_x(1)
+        def gather_side(j, a, b):
+            nc.scalar.activation(side[:, j, a:b], plane[j][:].indirect(entries(offs_t, 256 + a, 256 + b)), COPY)
+
+        for j in PLANE_ORDER:
+            if j != PLANE_ORDER[-1]:
+                gather_side(j, 0, 256)
+            gather_plane(j, *picks[0])
+            gather_plane(j, *picks[2])
+        for a in (0, P):
+            gather_side(PLANE_ORDER[-1], a, a + P)
+            src = side[:, :, a : a + P].rearrange("p j n -> p n j")
+            nc.gpsimd.tensor_scalar(xg[1][:, a : a + P, :], src, 1.0, 0.0, MULT, ADD)
+        weave_x("scalar", 0)
+        for u in range(2):
+            weave_w1("scalar", *W1_SCALAR[u])
+            weave_w1("vector", *W1_VECTOR[u])
         quant_x(0)
-        warm = take_bank(7)[:].rearrange("p t n -> p (t n)")[:, 0:256]
-        for rep in range(WARM_UPS):
-            nc.tensor.matmul_mx(
-                out=warm,
-                lhsT=xc[0][:, 0:P].bitcast(FP8X4),
-                lhsT_scale=xs[0][:, 0:P],
-                rhs=xc[0][:].bitcast(FP8X4),
-                rhs_scale=xs[0][:],
-                start=True,
-                stop=True,
-            )
-        gather_plane(PLANE_ORDER[-1], S // 2, S, T + 8)
-        for u in range(len(w1_parts)):
-            weave_w1(u)
         quant_w1(0, 2)
         quant_w1(2, 3)
         quant_w1(3, 4)
-        for m in range(2):
-            weave("scalar", w2g[:, m * P : (m + 1) * P, :], w2r[m], 0, P)
-
-        weave_x(2)
+        weave_x("scalar", 2)
+        weave("scalar", w2g[0][:], w2r[0][:])
         quant_x(1)
         quant_x(2)
-        for a, b, bank in CHUNKS[:6]:
-            layer1(a, b, bank)
-        relu_out("scalar", *CHUNKS[0][:2])
-        for a, b, bank in CHUNKS[6:]:
-            layer1(a, b, bank)
-        for c in (1, 3, 4, 6, 7):
-            relu_out("scalar", *CHUNKS[c][:2])
-        quant(w2c[:], w2s[:], w2g[:].rearrange("p n j -> p (n j)"))
+        weave("vector", w2g[1][:], w2r[1][:])
+        quant_w2(0)
+        quant_w2(1)
+        for c in range(8):
+            layer1(c)
+        for c in range(8):
+            relu_out(c)
 
-        relu_out("vector", *CHUNKS[2][:2])
-        relu_out("vector", *CHUNKS[5][:2])
+        for first, bank in ((0, 1), (512, 2), (768, 0)):
+            y_bank_for(0, first, bank)
         quant_h(0, 512)
-        layer2(0, 0, 512, 1)
+        layer2(0, 0, 0, 512)
         quant_h(512, 768)
+        layer2(0, 512, 512, 768)
         quant_h(768, 896)
-        layer2(0, 768, 896, 2)
+        layer2(0, 768, 768, 896)
         quant_h(896, 1024)
-        layer2(0, 896, 1024, 3)
-        layer2(0, 512, 768, 7)
+        layer2(0, 768, 896, 1024)
         y_out("scalar", 0, 0, 512)
-        y_out("vector", 0, 512, 768)
-        y_out("scalar", 0, 768, 896)
-        y_out("scalar", 0, 896, 1024)
-        layer2(1, 0, 512, 2)
-        layer2(1, 512, 1024, 3)
-        y_out("scalar", 1, 0, 512)
-        y_out("scalar", 1, 512, 1024)
+        y_out("scalar", 0, 512, 768)
+        y_out("vector", 0, 768, 1024)
+        for first, bank in ((0, 3), (512, 4)):
+            y_bank_for(1, first, bank)
+            layer2(1, first, first, first + 512)
+            y_out("scalar", 1, first, first + 512)
 
-        fetch(0, 0, 0, V)
-        fetch(0, 1, 0, V // 2)
-        fetch(0, 1, V // 2, V)
-        fetch(1, 0, 0, V)
-        turned = [take_bank(b) for b in (4, 5, 6, 7)]
-        for d in range(2):
-            for k in range(4):
-                nc.tensor.matmul(
-                    turned[k][:, 0, :],
-                    part[0][d][:, k * P : (k + 1) * P],
-                    ident[:],
-                    start=(d == 0),
-                    stop=(d == 1),
-                    is_transpose=True,
-                )
-        back = [take_bank(b) for b in (0, 1)]
-        for k in range(4):
-            nc.scalar.copy(turned_sum[:, k, :], turned[k][:, 0, :])
-            nc.tensor.transpose(back[k // 2][:, k % 2, :], turned_sum[:, k, :], ident[:])
-        for u in range(2):
-            cols = slice(2 * u * P, 2 * (u + 1) * P)
-            nc.scalar.copy(res[0][:, cols], back[u][:, 0:2, :].rearrange("p t n -> p (t n)"))
-            nc.scalar.dma_start(out=out[0:P, cols], in_=res[0][:, cols])
-        fetch(1, 1, 0, V // 2)
-        fetch(1, 1, V // 2, V)
-        finish(1, 0, V // 2)
-        finish(1, V // 2, V)
+        fetch_gated(0, 0, V)
+        fetch_gated(1, 0, V)
+        fetch_plain(0, 0, V)
+        gate_plain(0, 0, V)
+        finish(0, 0, V)
+        for a in (0, V // 2):
+            fetch_plain(1, a, a + V // 2)
+        for a in (0, V // 2):
+            gate_plain(1, a, a + V // 2)
+        for a in (0, V // 2):
+            finish(1, a, a + V // 2)

@@ -21,20 +21,18 @@ MAX = mybir.AluOpType.max
 FLOPS = 2 * S * H * K + 2 * S * N * H
 LIST_ROWS = 16
 
-PLANE_ORDER = (0, 2, 1, 3)
-SCALAR_ENTRIES = 256
+PLANE_ORDER = (0, 1, 2, 3)
+SIDE = (256, 640)
 LIST_CUTS = (0, 256, 512, 1024)
-W1_SCALAR = ((0, 128), (416, 512))
-W1_VECTOR = ((128, 256), (256, 416))
-VECTOR_CHUNKS = (3, 6)
+VECTOR_CHUNKS = (2, 4)
+WARM_UPS = 2
+W2_SCALAR = 192
 
 AT_W1G = 0
-AT_XC1 = AT_W1G
-AT_XC2 = AT_W1G + 1024
-AT_W1B = 4096
-AT_XC0 = AT_W1B
-AT_XG2 = AT_W1B + 1024
-AT_W2G1 = AT_XG2
+AT_XC1 = AT_W1G + 2048
+AT_XC2 = AT_W1G + 3072
+AT_HG3 = AT_W1G + 5120
+AT_Y1 = AT_HG3
 H_PIECES = (512, 256, P, P)
 
 
@@ -57,25 +55,25 @@ def tile_picked_sub_mlp_relu_sub_e_kernel(tc, xT, w1, w2, gate, offs, pos1, pos2
         offs_t = keep.tile([P, S // LIST_ROWS], U16, name="offs_t")
         pos_t = [keep.tile([P, V // LIST_ROWS], U16, name=f"pos_t{d}") for d in range(2)]
         plane = [own(f"plane{j}", [P, T], F32) for j in range(4)]
-        side = own("side", [P, 4, SCALAR_ENTRIES], BF16)
-        pairs = own("pairs", [P, 2, S, 2], BF16)
-        w1g = placed("w1g", [P, 4, P, 4], BF16, AT_W1G)
+        side = own("side", [P, 4, SIDE[1] - SIDE[0]], BF16)
+        w1g = [placed(f"w1g{a}", [P, 2, P, 4], BF16, AT_W1G + 2048 * a) for a in range(2)]
         picks = list(zip(LIST_CUTS[:-1], LIST_CUTS[1:]))
-        xg = [own("xg0", [P, 256, 4], BF16), own("xg1", [P, 256, 4], BF16), placed("xg2", [P, 512, 4], BF16, AT_XG2)]
-        xc = [placed("xc0", [P, 256], U32, AT_XC0), placed("xc1", [P, 256], U32, AT_XC1), placed("xc2", [P, 512], U32, AT_XC2)]
+        xg = own("xg", [P, S, 4], BF16)
+        xc = [own("xc0", [P, 256], U32), placed("xc1", [P, 256], U32, AT_XC1), placed("xc2", [P, 512], U32, AT_XC2)]
         xs = [own(f"xs{q}", [P, b - a], U8) for q, (a, b) in enumerate(picks)]
-        w1r = [own("w1r0", [P, 4, 256], F32), placed("w1r1", [P, 4, 256], F32, AT_W1B)]
+        w1r = own("w1r", [P, 4, H], F32)
         w1c = own("w1c", [P, H], U32)
         w1s = own("w1s", [P, H], U8)
-        w2r = [own(f"w2r{m}", [P, 4, P], F32) for m in range(2)]
-        w2g = [own("w2g0", [P, P, 4], BF16), placed("w2g1", [P, P, 4], BF16, AT_W2G1)]
+        w2r = own("w2r", [P, 4, N], F32)
+        w2g = own("w2g", [P, N, 4], BF16)
         w2c = own("w2c", [P, N], U32)
         w2s = own("w2s", [P, N], U8)
-        hg = [own(f"hg{i}", [P, n, 4], BF16) for i, n in enumerate(H_PIECES)]
+        hg = [own(f"hg{i}", [P, n, 4], BF16) for i, n in enumerate(H_PIECES[:3])]
+        hg.append(placed("hg3", [P, P, 4], BF16, AT_HG3))
         h_place = [(i, nth) for i, n in enumerate(H_PIECES) for nth in range(n // P)]
         hc = own("hc", [P, S], U32)
         hs = own("hs", [P, S], U8)
-        y = [own(f"y{m}", [P, S], F32) for m in range(2)]
+        y = [own("y0", [P, S], F32), placed("y1", [P, S], F32, AT_Y1)]
         gt = own("gt", [P, 2, V], F32)
         plain = [own(f"plain{m}", [P, V], F32) for m in range(2)]
         part = [[own(f"part{m}{d}", [P, V], F32) for d in range(2)] for m in range(2)]
@@ -87,10 +85,8 @@ def tile_picked_sub_mlp_relu_sub_e_kernel(tc, xT, w1, w2, gate, offs, pos1, pos2
             nc.sync.dma_start(out=plane[j][:], in_=x4[:, j, :])
             if j == PLANE_ORDER[0]:
                 nc.sync.dma_start(out=offs_t[:], in_=offs)
-        for u in range(2):
-            nc.sync.dma_start(out=w1r[u][:], in_=w14[:, :, 256 * u : 256 * (u + 1)])
-        for m in range(2):
-            nc.sync.dma_start(out=w2r[m][:], in_=w2.rearrange("(p j) n -> p j n", j=4)[:, :, m * P : (m + 1) * P])
+        nc.sync.dma_start(out=w1r[:], in_=w14)
+        nc.sync.dma_start(out=w2r[:], in_=w2.rearrange("(p j) n -> p j n", j=4))
         nc.sync.dma_start(out=pos_t[0][:], in_=pos1)
         nc.sync.dma_start(out=pos_t[1][:], in_=pos2)
         nc.sync.dma_start(out=gt[:], in_=gate[:, 0:P, :].rearrange("d p v -> p d v"))
@@ -101,14 +97,9 @@ def tile_picked_sub_mlp_relu_sub_e_kernel(tc, xT, w1, w2, gate, offs, pos1, pos2
             else:
                 nc.vector.tensor_copy(dst, src)
 
-        def weave_w1(engine, a, b):
-            u = a // 256
-            src = w1r[u][:, :, a - 256 * u : b - 256 * u]
-            dst = w1g[:, :, a // 4 : b // 4, :]
-            if engine == "gpsimd":
-                nc.gpsimd.tensor_scalar(dst, src.rearrange("p j (m t) -> p t m j", t=4), 1.0, 0.0, MULT, ADD)
-            else:
-                copy(engine, dst.rearrange("p t m j -> p m j t"), src.rearrange("p j (m t) -> p m j t", t=4))
+        def weave_w1(engine, t0, t1):
+            src = w1r[:].rearrange("p j (m t) -> p m j t", t=4)[:, :, :, t0:t1]
+            copy(engine, w1g[t0 // 2][:].rearrange("p t m j -> p m j t"), src)
 
         def weave(engine, dst, src):
             copy(engine, dst.rearrange("p (c i) j -> p c j i", i=4), src.rearrange("p j (c i) -> p c j i", i=4))
@@ -116,21 +107,13 @@ def tile_picked_sub_mlp_relu_sub_e_kernel(tc, xT, w1, w2, gate, offs, pos1, pos2
         def quant(words, scales, woven):
             nc.vector.quantize_mx(out=words.bitcast(FP8X4), scales=scales, in_=woven)
 
-        def weave_x(engine, q):
-            a, b = picks[q]
-            dst = xg[q][:].rearrange("p n j -> p (n j)").bitcast(U32).rearrange("p (n u) -> p n u", u=2)
-            words = pairs[:].rearrange("p u n e -> p u (n e)").bitcast(U32)
-            copy(engine, dst, words[:, :, a:b].rearrange("p u n -> p n u"))
-
         def quant_x(q):
-            quant(xc[q][:], xs[q][:], xg[q][:].rearrange("p n j -> p (n j)"))
+            a, b = picks[q]
+            quant(xc[q][:], xs[q][:], xg[:, a:b, :].rearrange("p n j -> p (n j)"))
 
         def quant_w1(t0, t1):
-            flat = w1g[:].rearrange("p t m j -> p (t m j)")
-            quant(w1c[:, t0 * P : t1 * P], w1s[:, t0 * P : t1 * P], flat[:, 4 * t0 * P : 4 * t1 * P])
-
-        def quant_w2(m):
-            quant(w2c[:, m * P : (m + 1) * P], w2s[:, m * P : (m + 1) * P], w2g[m][:].rearrange("p n j -> p (n j)"))
+            flat = w1g[t0 // 2][:].rearrange("p t m j -> p (t m j)")
+            quant(w1c[:, t0 * P : t1 * P], w1s[:, t0 * P : t1 * P], flat)
 
         def quant_h(a, b):
             quant(hc[:, a:b], hs[:, a:b], hg[h_place[a // P][0]][:].rearrange("p n j -> p (n j)"))
@@ -139,7 +122,7 @@ def tile_picked_sub_mlp_relu_sub_e_kernel(tc, xT, w1, w2, gate, offs, pos1, pos2
             return list_tile[:, a // LIST_ROWS : b // LIST_ROWS]
 
         def gather_plane(j, a, b):
-            nc.vector.tensor_copy(pairs[:, j // 2, a:b, j % 2], plane[j][:].indirect(entries(offs_t, a, b)))
+            nc.vector.tensor_copy(xg[:, a:b, j], plane[j][:].indirect(entries(offs_t, a, b)))
 
         h_bank = {}
         y_bank = {}
@@ -200,32 +183,37 @@ def tile_picked_sub_mlp_relu_sub_e_kernel(tc, xT, w1, w2, gate, offs, pos1, pos2
             nc.sync.dma_start(out=out[m * P : (m + 1) * P, a:b], in_=res[m][:, a:b])
 
         def gather_side(j, a, b):
-            nc.scalar.activation(side[:, j, a:b], plane[j][:].indirect(entries(offs_t, 256 + a, 256 + b)), COPY)
+            staged = side[:, j, a - SIDE[0] : b - SIDE[0]]
+            nc.scalar.activation(staged, plane[j][:].indirect(entries(offs_t, a, b)), COPY)
+            nc.gpsimd.tensor_scalar(xg[:, a:b, j], staged, 1.0, 0.0, MULT, ADD)
 
-        for j in PLANE_ORDER:
-            if j != PLANE_ORDER[-1]:
-                gather_side(j, 0, 256)
-            gather_plane(j, *picks[0])
-            gather_plane(j, *picks[2])
-        for a in (0, P):
-            gather_side(PLANE_ORDER[-1], a, a + P)
-            src = side[:, :, a : a + P].rearrange("p j n -> p n j")
-            nc.gpsimd.tensor_scalar(xg[1][:, a : a + P, :], src, 1.0, 0.0, MULT, ADD)
-        weave_x("scalar", 0)
-        for u in range(2):
-            weave_w1("scalar", *W1_SCALAR[u])
-            weave_w1("vector", *W1_VECTOR[u])
+        for j in range(4):
+            gather_plane(j, 0, SIDE[0])
+            gather_plane(j, SIDE[1], S)
+            step = P if j == 3 else SIDE[1] - SIDE[0]
+            for a in range(SIDE[0], SIDE[1], step):
+                gather_side(j, a, a + step)
         quant_x(0)
+        warm = take_bank(7)[:].rearrange("p t n -> p (t n)")[:, 0:256]
+        for rep in range(WARM_UPS):
+            nc.tensor.matmul_mx(
+                out=warm,
+                lhsT=xc[0][:, 0:P].bitcast(FP8X4),
+                lhsT_scale=xs[0][:, 0:P],
+                rhs=xc[0][:].bitcast(FP8X4),
+                rhs_scale=xs[0][:],
+                start=True,
+                stop=True,
+            )
+        weave_w1("vector", 0, 2)
+        weave_w1("scalar", 2, 4)
         quant_w1(0, 2)
-        quant_w1(2, 3)
-        quant_w1(3, 4)
-        weave_x("scalar", 2)
-        weave("scalar", w2g[0][:], w2r[0][:])
+        quant_w1(2, 4)
         quant_x(1)
+        weave("scalar", w2g[:, 0:W2_SCALAR, :], w2r[:, :, 0:W2_SCALAR])
         quant_x(2)
-        weave("vector", w2g[1][:], w2r[1][:])
-        quant_w2(0)
-        quant_w2(1)
+        weave("vector", w2g[:, W2_SCALAR:N, :], w2r[:, :, W2_SCALAR:N])
+        quant(w2c[:], w2s[:], w2g[:].rearrange("p n j -> p (n j)"))
         for c in range(8):
             layer1(c)
         for c in range(8):

@@ -22,7 +22,9 @@ FLOPS = 2 * S * H * K + 2 * S * N * H
 LIST_ROWS = 16
 
 PLANE_ORDER = (0, 1, 2, 3)
-SIDE = (256, 640)
+SIDE = (256, 704)
+PLACED_BY_GPSIMD = 544
+LAST_CUTS = (256, 384, 544)
 LIST_CUTS = (0, 256, 512, 1024)
 VECTOR_CHUNKS = (2, 4)
 WARM_UPS = 2
@@ -182,17 +184,25 @@ def tile_picked_sub_mlp_relu_sub_e_kernel(tc, xT, w1, w2, gate, offs, pos1, pos2
             nc.vector.tensor_tensor(res[m][:, a:b], part[m][0][:, a:b], part[m][1][:, a:b], ADD)
             nc.sync.dma_start(out=out[m * P : (m + 1) * P, a:b], in_=res[m][:, a:b])
 
+        spare = own("spare", [P, 2], F32)
+        nc.gpsimd.memset(spare[:, 0:1], 0.0)
+        nc.scalar.activation(spare[:, 1:2], spare[:, 0:1], COPY)
+
         def gather_side(j, a, b):
             staged = side[:, j, a - SIDE[0] : b - SIDE[0]]
             nc.scalar.activation(staged, plane[j][:].indirect(entries(offs_t, a, b)), COPY)
-            nc.gpsimd.tensor_scalar(xg[:, a:b, j], staged, 1.0, 0.0, MULT, ADD)
+            if b <= PLACED_BY_GPSIMD:
+                nc.gpsimd.tensor_scalar(xg[:, a:b, j], staged, 1.0, 0.0, MULT, ADD)
+            else:
+                nc.scalar.copy(xg[:, a:b, j], staged)
 
         for j in range(4):
             gather_plane(j, 0, SIDE[0])
             gather_plane(j, SIDE[1], S)
-            step = P if j == 3 else SIDE[1] - SIDE[0]
-            for a in range(SIDE[0], SIDE[1], step):
-                gather_side(j, a, a + step)
+            cuts = LAST_CUTS if j == 3 else (SIDE[0], PLACED_BY_GPSIMD)
+            for a, b in zip(cuts[:-1], cuts[1:]):
+                gather_side(j, a, b)
+            gather_side(j, PLACED_BY_GPSIMD, SIDE[1])
         quant_x(0)
         warm = take_bank(7)[:].rearrange("p t n -> p (t n)")[:, 0:256]
         for rep in range(WARM_UPS):
@@ -219,7 +229,7 @@ def tile_picked_sub_mlp_relu_sub_e_kernel(tc, xT, w1, w2, gate, offs, pos1, pos2
         for c in range(8):
             relu_out(c)
 
-        for first, bank in ((0, 1), (512, 2), (768, 0)):
+        for first, bank in ((0, 1), (512, 2), (768, 0), (896, 5)):
             y_bank_for(0, first, bank)
         quant_h(0, 512)
         layer2(0, 0, 0, 512)
@@ -228,10 +238,11 @@ def tile_picked_sub_mlp_relu_sub_e_kernel(tc, xT, w1, w2, gate, offs, pos1, pos2
         quant_h(768, 896)
         layer2(0, 768, 768, 896)
         quant_h(896, 1024)
-        layer2(0, 768, 896, 1024)
+        layer2(0, 896, 896, 1024)
         y_out("scalar", 0, 0, 512)
-        y_out("scalar", 0, 512, 768)
-        y_out("vector", 0, 768, 1024)
+        y_out("vector", 0, 512, 768)
+        y_out("scalar", 0, 768, 896)
+        y_out("scalar", 0, 896, 1024)
         for first, bank in ((0, 3), (512, 4)):
             y_bank_for(1, first, bank)
             layer2(1, first, first, first + 512)
@@ -240,11 +251,11 @@ def tile_picked_sub_mlp_relu_sub_e_kernel(tc, xT, w1, w2, gate, offs, pos1, pos2
         fetch_gated(0, 0, V)
         fetch_gated(1, 0, V)
         fetch_plain(0, 0, V)
-        gate_plain(0, 0, V)
-        finish(0, 0, V)
         for a in (0, V // 2):
             fetch_plain(1, a, a + V // 2)
-        for a in (0, V // 2):
-            gate_plain(1, a, a + V // 2)
+        gate_plain(0, 0, V)
+        gate_plain(1, 0, V // 2)
+        finish(0, 0, V)
+        gate_plain(1, V // 2, V)
         for a in (0, V // 2):
             finish(1, a, a + V // 2)

@@ -26,15 +26,23 @@ SIDE = (256, 704)
 PLACED_BY_GPSIMD = 544
 LAST_CUTS = (256, 384, 544)
 LIST_CUTS = (0, 256, 512, 1024)
-VECTOR_CHUNKS = (2, 4)
+CHUNKS = (
+    (0, 128, 0, "scalar"), (128, 256, 1, "scalar"), (256, 384, 2, "vector"), (384, 512, 3, "scalar"),
+    (512, 640, 4, "vector"), (640, 768, 5, "scalar"), (768, 896, 6, "scalar"), (896, 960, 0, "vector"),
+    (960, 1024, 7, "scalar"),
+)
 WARM_UPS = 2
+W1_FIRST = 88
+W1_SECOND = 80
 W2_SCALAR = 192
 
 AT_W1G = 0
 AT_XC1 = AT_W1G + 2048
 AT_XC2 = AT_W1G + 3072
-AT_HG3 = AT_W1G + 5120
-AT_Y1 = AT_HG3
+AT_HG0 = AT_W1G + 5120
+AT_HG3 = AT_HG0
+AT_W2C0 = AT_HG0 + 4096
+AT_Y1 = AT_W2C0
 H_PIECES = (512, 256, P, P)
 
 
@@ -68,10 +76,14 @@ def tile_picked_sub_mlp_relu_sub_e_kernel(tc, xT, w1, w2, gate, offs, pos1, pos2
         w1s = own("w1s", [P, H], U8)
         w2r = own("w2r", [P, 4, N], F32)
         w2g = own("w2g", [P, N, 4], BF16)
-        w2c = own("w2c", [P, N], U32)
-        w2s = own("w2s", [P, N], U8)
-        hg = [own(f"hg{i}", [P, n, 4], BF16) for i, n in enumerate(H_PIECES[:3])]
-        hg.append(placed("hg3", [P, P, 4], BF16, AT_HG3))
+        w2c = [placed("w2c0", [P, P], U32, AT_W2C0), own("w2c1", [P, P], U32)]
+        w2s = [own(f"w2s{m}", [P, P], U8) for m in range(2)]
+        hg = [
+            placed("hg0", [P, 512, 4], BF16, AT_HG0),
+            own("hg1", [P, 256, 4], BF16),
+            own("hg2", [P, P, 4], BF16),
+            placed("hg3", [P, P, 4], BF16, AT_HG3),
+        ]
         h_place = [(i, nth) for i, n in enumerate(H_PIECES) for nth in range(n // P)]
         hc = own("hc", [P, S], U32)
         hs = own("hs", [P, S], U8)
@@ -99,9 +111,9 @@ def tile_picked_sub_mlp_relu_sub_e_kernel(tc, xT, w1, w2, gate, offs, pos1, pos2
             else:
                 nc.vector.tensor_copy(dst, src)
 
-        def weave_w1(engine, t0, t1):
-            src = w1r[:].rearrange("p j (m t) -> p m j t", t=4)[:, :, :, t0:t1]
-            copy(engine, w1g[t0 // 2][:].rearrange("p t m j -> p m j t"), src)
+        def weave_w1(engine, t0, t1, a, b):
+            src = w1r[:].rearrange("p j (m t) -> p m j t", t=4)[:, a:b, :, t0:t1]
+            copy(engine, w1g[t0 // 2][:, :, a:b, :].rearrange("p t m j -> p m j t"), src)
 
         def weave(engine, dst, src):
             copy(engine, dst.rearrange("p (c i) j -> p c j i", i=4), src.rearrange("p j (c i) -> p c j i", i=4))
@@ -113,12 +125,14 @@ def tile_picked_sub_mlp_relu_sub_e_kernel(tc, xT, w1, w2, gate, offs, pos1, pos2
             a, b = picks[q]
             quant(xc[q][:], xs[q][:], xg[:, a:b, :].rearrange("p n j -> p (n j)"))
 
-        def quant_w1(t0, t1):
-            flat = w1g[t0 // 2][:].rearrange("p t m j -> p (t m j)")
-            quant(w1c[:, t0 * P : t1 * P], w1s[:, t0 * P : t1 * P], flat)
+        def quant_w1(t):
+            flat = w1g[t // 2][:, t % 2, :, :].rearrange("p m j -> p (m j)")
+            quant(w1c[:, t * P : (t + 1) * P], w1s[:, t * P : (t + 1) * P], flat)
 
         def quant_h(a, b):
-            quant(hc[:, a:b], hs[:, a:b], hg[h_place[a // P][0]][:].rearrange("p n j -> p (n j)"))
+            piece, nth = h_place[a // P]
+            woven = hg[piece][:, nth * P : nth * P + b - a, :]
+            quant(hc[:, a:b], hs[:, a:b], woven.rearrange("p n j -> p (n j)"))
 
         def entries(list_tile, a, b):
             return list_tile[:, a // LIST_ROWS : b // LIST_ROWS]
@@ -129,14 +143,13 @@ def tile_picked_sub_mlp_relu_sub_e_kernel(tc, xT, w1, w2, gate, offs, pos1, pos2
         h_bank = {}
         y_bank = {}
 
-        def layer1(c):
-            a, b = c * P, (c + 1) * P
-            h_bank[c] = take_bank(c)
+        def layer1(a, b, bank):
+            h_bank[a] = take_bank(bank)[:, :, 0 : b - a]
             q = max(i for i, (lo, hi) in enumerate(picks) if lo <= a)
             cols = slice(a - picks[q][0], b - picks[q][0])
             for t in range(4):
                 nc.tensor.matmul_mx(
-                    out=h_bank[c][:, t, :],
+                    out=h_bank[a][:, t, :],
                     lhsT=w1c[:, t * P : (t + 1) * P].bitcast(FP8X4),
                     lhsT_scale=w1s[:, t * P : (t + 1) * P],
                     rhs=xc[q][:, cols].bitcast(FP8X4),
@@ -145,11 +158,12 @@ def tile_picked_sub_mlp_relu_sub_e_kernel(tc, xT, w1, w2, gate, offs, pos1, pos2
                     stop=True,
                 )
 
-        def relu_out(c):
-            piece, nth = h_place[c]
-            dst = hg[piece][:, nth * P : (nth + 1) * P, :]
-            src = h_bank[c][:].rearrange("p t n -> p n t")
-            if c in VECTOR_CHUNKS:
+        def relu_out(a, b, engine):
+            piece, nth = h_place[a // P]
+            first = nth * P + a % P
+            dst = hg[piece][:, first : first + b - a, :]
+            src = h_bank[a].rearrange("p t n -> p n t")
+            if engine == "vector":
                 nc.vector.tensor_scalar(dst, src, 0.0, None, MAX)
             else:
                 nc.scalar.activation(dst, src, RELU)
@@ -160,8 +174,8 @@ def tile_picked_sub_mlp_relu_sub_e_kernel(tc, xT, w1, w2, gate, offs, pos1, pos2
         def layer2(m, first, a, b):
             nc.tensor.matmul_mx(
                 out=y_bank[m, first][:, a - first : b - first],
-                lhsT=w2c[:, m * P : (m + 1) * P].bitcast(FP8X4),
-                lhsT_scale=w2s[:, m * P : (m + 1) * P],
+                lhsT=w2c[m][:].bitcast(FP8X4),
+                lhsT_scale=w2s[m][:],
                 rhs=hc[:, a:b].bitcast(FP8X4),
                 rhs_scale=hs[:, a:b],
                 start=True,
@@ -215,23 +229,31 @@ def tile_picked_sub_mlp_relu_sub_e_kernel(tc, xT, w1, w2, gate, offs, pos1, pos2
                 start=True,
                 stop=True,
             )
-        weave_w1("vector", 0, 2)
-        weave_w1("scalar", 2, 4)
-        quant_w1(0, 2)
-        quant_w1(2, 4)
+        weave_w1("vector", 0, 2, 0, W1_FIRST)
+        weave_w1("scalar", 0, 2, W1_FIRST, P)
+        weave_w1("vector", 2, 4, W1_SECOND, P)
+        weave_w1("scalar", 2, 4, 0, W1_SECOND)
+        for t in range(4):
+            quant_w1(t)
         quant_x(1)
         weave("scalar", w2g[:, 0:W2_SCALAR, :], w2r[:, :, 0:W2_SCALAR])
-        quant_x(2)
         weave("vector", w2g[:, W2_SCALAR:N, :], w2r[:, :, W2_SCALAR:N])
-        quant(w2c[:], w2s[:], w2g[:].rearrange("p n j -> p (n j)"))
-        for c in range(8):
-            layer1(c)
-        for c in range(8):
-            relu_out(c)
+        quant_x(2)
+        for m in range(2):
+            quant(w2c[m][:], w2s[m][:], w2g[:, m * P : (m + 1) * P, :].rearrange("p n j -> p (n j)"))
+        for a, b, bank, engine in CHUNKS[:7]:
+            layer1(a, b, bank)
+            relu_out(a, b, engine)
+            if b == 384:
+                quant_h(0, 256)
+        for a, b, bank, engine in CHUNKS[7:]:
+            layer1(a, b, bank)
 
-        for first, bank in ((0, 1), (512, 2), (768, 0), (896, 5)):
+        for first, bank in ((0, 1), (512, 2), (768, 5), (896, 6)):
             y_bank_for(0, first, bank)
-        quant_h(0, 512)
+        quant_h(256, 512)
+        for a, b, bank, engine in CHUNKS[7:]:
+            relu_out(a, b, engine)
         layer2(0, 0, 0, 512)
         quant_h(512, 768)
         layer2(0, 512, 512, 768)

@@ -25,20 +25,22 @@ PLANE_ORDER = (0, 1, 2, 3)
 SIDE = (256, 704)
 PLACED_BY_GPSIMD = 544
 LAST_CUTS = (256, 384, 544)
-LIST_CUTS = (0, 256, 512, 1024)
+LIST_CUTS = (0, 128, 256, 512, 1024)
 CHUNKS = (
     (0, 128, 0, "scalar"), (128, 256, 1, "scalar"), (256, 384, 2, "vector"), (384, 512, 3, "scalar"),
     (512, 640, 4, "vector"), (640, 768, 5, "scalar"), (768, 896, 6, "scalar"), (896, 960, 0, "vector"),
     (960, 1024, 7, "scalar"),
 )
-WARM_UPS = 2
+WARM_UPS = 4
+EARLY_SIDE_END = 736
 W1_FIRST = 88
 W1_SECOND = 80
 W2_SCALAR = 192
 
 AT_W1G = 0
-AT_XC1 = AT_W1G + 2048
-AT_XC2 = AT_W1G + 3072
+AT_XC1 = AT_W1G
+AT_XC2 = AT_W1G + 2048
+AT_XC3 = AT_W1G + 3072
 AT_HG0 = AT_W1G + 5120
 AT_HG3 = AT_HG0
 AT_W2C0 = AT_HG0 + 4096
@@ -65,11 +67,16 @@ def tile_picked_sub_mlp_relu_sub_e_kernel(tc, xT, w1, w2, gate, offs, pos1, pos2
         offs_t = keep.tile([P, S // LIST_ROWS], U16, name="offs_t")
         pos_t = [keep.tile([P, V // LIST_ROWS], U16, name=f"pos_t{d}") for d in range(2)]
         plane = [own(f"plane{j}", [P, T], F32) for j in range(4)]
-        side = own("side", [P, 4, SIDE[1] - SIDE[0]], BF16)
+        side = own("side", [P, 4, EARLY_SIDE_END - SIDE[0]], BF16)
         w1g = [placed(f"w1g{a}", [P, 2, P, 4], BF16, AT_W1G + 2048 * a) for a in range(2)]
         picks = list(zip(LIST_CUTS[:-1], LIST_CUTS[1:]))
         xg = own("xg", [P, S, 4], BF16)
-        xc = [own("xc0", [P, 256], U32), placed("xc1", [P, 256], U32, AT_XC1), placed("xc2", [P, 512], U32, AT_XC2)]
+        xc = [
+            own("xc0", [P, P], U32),
+            placed("xc1", [P, P], U32, AT_XC1),
+            placed("xc2", [P, 256], U32, AT_XC2),
+            placed("xc3", [P, 512], U32, AT_XC3),
+        ]
         xs = [own(f"xs{q}", [P, b - a], U8) for q, (a, b) in enumerate(picks)]
         w1r = own("w1r", [P, 4, H], F32)
         w1c = own("w1c", [P, H], U32)
@@ -131,7 +138,8 @@ def tile_picked_sub_mlp_relu_sub_e_kernel(tc, xT, w1, w2, gate, offs, pos1, pos2
 
         def quant_h(a, b):
             piece, nth = h_place[a // P]
-            woven = hg[piece][:, nth * P : nth * P + b - a, :]
+            first = nth * P + a % P
+            woven = hg[piece][:, first : first + b - a, :]
             quant(hc[:, a:b], hs[:, a:b], woven.rearrange("p n j -> p (n j)"))
 
         def entries(list_tile, a, b):
@@ -212,13 +220,14 @@ def tile_picked_sub_mlp_relu_sub_e_kernel(tc, xT, w1, w2, gate, offs, pos1, pos2
 
         for j in range(4):
             gather_plane(j, 0, SIDE[0])
-            gather_plane(j, SIDE[1], S)
+            side_end = EARLY_SIDE_END if j < 2 else SIDE[1]
+            gather_plane(j, side_end, S)
             cuts = LAST_CUTS if j == 3 else (SIDE[0], PLACED_BY_GPSIMD)
             for a, b in zip(cuts[:-1], cuts[1:]):
                 gather_side(j, a, b)
-            gather_side(j, PLACED_BY_GPSIMD, SIDE[1])
+            gather_side(j, PLACED_BY_GPSIMD, side_end)
         quant_x(0)
-        warm = take_bank(7)[:].rearrange("p t n -> p (t n)")[:, 0:256]
+        warm = take_bank(7)[:].rearrange("p t n -> p (t n)")[:, 0:P]
         for rep in range(WARM_UPS):
             nc.tensor.matmul_mx(
                 out=warm,
@@ -235,10 +244,12 @@ def tile_picked_sub_mlp_relu_sub_e_kernel(tc, xT, w1, w2, gate, offs, pos1, pos2
         weave_w1("scalar", 2, 4, 0, W1_SECOND)
         for t in range(4):
             quant_w1(t)
-        quant_x(1)
+            if t == 1:
+                quant_x(1)
         weave("scalar", w2g[:, 0:W2_SCALAR, :], w2r[:, :, 0:W2_SCALAR])
         weave("vector", w2g[:, W2_SCALAR:N, :], w2r[:, :, W2_SCALAR:N])
         quant_x(2)
+        quant_x(3)
         for m in range(2):
             quant(w2c[m][:], w2s[m][:], w2g[:, m * P : (m + 1) * P, :].rearrange("p n j -> p (n j)"))
         for a, b, bank, engine in CHUNKS[:7]:
@@ -249,22 +260,24 @@ def tile_picked_sub_mlp_relu_sub_e_kernel(tc, xT, w1, w2, gate, offs, pos1, pos2
         for a, b, bank, engine in CHUNKS[7:]:
             layer1(a, b, bank)
 
-        for first, bank in ((0, 1), (512, 2), (768, 5), (896, 6)):
+        for first, bank in ((0, 1), (512, 2), (768, 5), (960, 6)):
             y_bank_for(0, first, bank)
         quant_h(256, 512)
-        for a, b, bank, engine in CHUNKS[7:]:
-            relu_out(a, b, engine)
         layer2(0, 0, 0, 512)
         quant_h(512, 768)
+        for a, b, bank, engine in CHUNKS[7:]:
+            relu_out(a, b, engine)
         layer2(0, 512, 512, 768)
         quant_h(768, 896)
         layer2(0, 768, 768, 896)
-        quant_h(896, 1024)
-        layer2(0, 896, 896, 1024)
+        quant_h(896, 960)
+        layer2(0, 768, 896, 960)
+        quant_h(960, 1024)
+        layer2(0, 960, 960, 1024)
         y_out("scalar", 0, 0, 512)
         y_out("vector", 0, 512, 768)
-        y_out("scalar", 0, 768, 896)
-        y_out("scalar", 0, 896, 1024)
+        y_out("scalar", 0, 768, 960)
+        y_out("scalar", 0, 960, 1024)
         for first, bank in ((0, 3), (512, 4)):
             y_bank_for(1, first, bank)
             layer2(1, first, first, first + 512)

@@ -32,7 +32,6 @@ CHUNKS = (
     (960, 1024, 7, "scalar"),
 )
 WARM_UPS = 4
-EARLY_SIDE_END = 736
 W1_FIRST = 88
 W1_SECOND = 80
 W2_SCALAR = 192
@@ -67,7 +66,7 @@ def tile_picked_sub_mlp_relu_sub_e_kernel(tc, xT, w1, w2, gate, offs, pos1, pos2
         offs_t = keep.tile([P, S // LIST_ROWS], U16, name="offs_t")
         pos_t = [keep.tile([P, V // LIST_ROWS], U16, name=f"pos_t{d}") for d in range(2)]
         plane = [own(f"plane{j}", [P, T], F32) for j in range(4)]
-        side = own("side", [P, 4, EARLY_SIDE_END - SIDE[0]], BF16)
+        side = own("side", [P, 4, SIDE[1] - SIDE[0]], BF16)
         w1g = [placed(f"w1g{a}", [P, 2, P, 4], BF16, AT_W1G + 2048 * a) for a in range(2)]
         picks = list(zip(LIST_CUTS[:-1], LIST_CUTS[1:]))
         xg = own("xg", [P, S, 4], BF16)
@@ -220,12 +219,11 @@ def tile_picked_sub_mlp_relu_sub_e_kernel(tc, xT, w1, w2, gate, offs, pos1, pos2
 
         for j in range(4):
             gather_plane(j, 0, SIDE[0])
-            side_end = EARLY_SIDE_END if j < 2 else SIDE[1]
-            gather_plane(j, side_end, S)
+            gather_plane(j, SIDE[1], S)
             cuts = LAST_CUTS if j == 3 else (SIDE[0], PLACED_BY_GPSIMD)
             for a, b in zip(cuts[:-1], cuts[1:]):
                 gather_side(j, a, b)
-            gather_side(j, PLACED_BY_GPSIMD, side_end)
+            gather_side(j, PLACED_BY_GPSIMD, SIDE[1])
         quant_x(0)
         warm = take_bank(7)[:].rearrange("p t n -> p (t n)")[:, 0:P]
         for rep in range(WARM_UPS):

@@ -32,15 +32,15 @@ CHUNKS = (
     (960, 1024, 7, "scalar"),
 )
 WARM_UPS = 4
-W1_FIRST = 88
+W1_FIRST = 72
 W1_SECOND = 80
-W2_SCALAR = 192
 
 AT_W1G = 0
 AT_XC1 = AT_W1G
-AT_XC2 = AT_W1G + 2048
-AT_XC3 = AT_W1G + 3072
-AT_HG0 = AT_W1G + 5120
+AT_W1R = AT_W1G + 4096
+AT_XC2 = AT_W1R
+AT_XC3 = AT_W1R + 1024
+AT_HG0 = AT_W1R + 8192
 AT_HG3 = AT_HG0
 AT_W2C0 = AT_HG0 + 4096
 AT_Y1 = AT_W2C0
@@ -77,7 +77,7 @@ def tile_picked_sub_mlp_relu_sub_e_kernel(tc, xT, w1, w2, gate, offs, pos1, pos2
             placed("xc3", [P, 512], U32, AT_XC3),
         ]
         xs = [own(f"xs{q}", [P, b - a], U8) for q, (a, b) in enumerate(picks)]
-        w1r = own("w1r", [P, 4, H], F32)
+        w1r = placed("w1r", [P, 4, H], F32, AT_W1R)
         w1c = own("w1c", [P, H], U32)
         w1s = own("w1s", [P, H], U8)
         w2r = own("w2r", [P, 4, N], F32)
@@ -244,8 +244,7 @@ def tile_picked_sub_mlp_relu_sub_e_kernel(tc, xT, w1, w2, gate, offs, pos1, pos2
             quant_w1(t)
             if t == 1:
                 quant_x(1)
-        weave("scalar", w2g[:, 0:W2_SCALAR, :], w2r[:, :, 0:W2_SCALAR])
-        weave("vector", w2g[:, W2_SCALAR:N, :], w2r[:, :, W2_SCALAR:N])
+        weave("scalar", w2g[:], w2r[:])
         quant_x(2)
         quant_x(3)
         for m in range(2):

@@ -23,8 +23,8 @@ LIST_ROWS = 16
 
 PLANE_ORDER = (0, 1, 2, 3)
 SIDE = (256, 704)
-PLACED_BY_GPSIMD = 544
-LAST_CUTS = (256, 384, 544)
+GPSIMD_CUTS = ((256, 480), (256, 320, 480))
+SCALAR_CUTS = ((480, 704), (480, 608, 704))
 LIST_CUTS = (0, 128, 256, 512, 1024)
 CHUNKS = (
     (0, 128, 0, "scalar"), (128, 256, 1, "scalar"), (256, 384, 2, "vector"), (384, 512, 3, "scalar"),
@@ -205,25 +205,30 @@ def tile_picked_sub_mlp_relu_sub_e_kernel(tc, xT, w1, w2, gate, offs, pos1, pos2
             nc.vector.tensor_tensor(res[m][:, a:b], part[m][0][:, a:b], part[m][1][:, a:b], ADD)
             nc.sync.dma_start(out=out[m * P : (m + 1) * P, a:b], in_=res[m][:, a:b])
 
-        spare = own("spare", [P, 2], F32)
-        nc.gpsimd.memset(spare[:, 0:1], 0.0)
-        nc.scalar.activation(spare[:, 1:2], spare[:, 0:1], COPY)
-
-        def gather_side(j, a, b):
+        def stage(j, a, b):
             staged = side[:, j, a - SIDE[0] : b - SIDE[0]]
             nc.scalar.activation(staged, plane[j][:].indirect(entries(offs_t, a, b)), COPY)
-            if b <= PLACED_BY_GPSIMD:
-                nc.gpsimd.tensor_scalar(xg[:, a:b, j], staged, 1.0, 0.0, MULT, ADD)
+
+        def place(engine, u, a, b):
+            dst = xg[:, a:b, 2 * u : 2 * u + 2]
+            src = side[:, 2 * u : 2 * u + 2, a - SIDE[0] : b - SIDE[0]].rearrange("p e n -> p n e")
+            if engine == "gpsimd":
+                nc.gpsimd.tensor_scalar(dst, src, 1.0, 0.0, MULT, ADD)
             else:
-                nc.scalar.copy(xg[:, a:b, j], staged)
+                nc.scalar.copy(dst, src)
 
         for j in range(4):
             gather_plane(j, 0, SIDE[0])
             gather_plane(j, SIDE[1], S)
-            cuts = LAST_CUTS if j == 3 else (SIDE[0], PLACED_BY_GPSIMD)
-            for a, b in zip(cuts[:-1], cuts[1:]):
-                gather_side(j, a, b)
-            gather_side(j, PLACED_BY_GPSIMD, SIDE[1])
+            if j % 2 == 0:
+                stage(j, *SIDE)
+            else:
+                for engine, cuts in (("gpsimd", GPSIMD_CUTS[j // 2]), ("scalar", SCALAR_CUTS[j // 2])):
+                    pieces = list(zip(cuts[:-1], cuts[1:]))
+                    for a, b in pieces:
+                        stage(j, a, b)
+                    for a, b in pieces:
+                        place(engine, j // 2, a, b)
         quant_x(0)
         warm = take_bank(7)[:].rearrange("p t n -> p (t n)")[:, 0:P]
         for rep in range(WARM_UPS):

@@ -31,6 +31,8 @@ CHUNKS = (
     (512, 640, 4, "vector"), (640, 768, 5, "scalar"), (768, 896, 6, "scalar"), (896, 960, 0, "vector"),
     (960, 1024, 7, "scalar"),
 )
+PLANE_PITCH = 50 * 1024
+PLANE_PLACE = (0, 2, 1, 3)
 WARM_UPS = 4
 W1_FIRST = 72
 W1_SECOND = 80
@@ -52,6 +54,7 @@ def tile_picked_sub_mlp_relu_sub_e_kernel(tc, xT, w1, w2, gate, offs, pos1, pos2
     with ExitStack() as ctx:
         keep = ctx.enter_context(tc.tile_pool(name="keep", bufs=1))
         reuse = ctx.enter_context(tc.tile_pool(name="reuse", bufs=1))
+        spread = ctx.enter_context(tc.tile_pool(name="spread", bufs=1))
         psum = ctx.enter_context(tc.psum_pool(name="psum", bufs=1))
 
         def own(name, shape, dtype):
@@ -65,7 +68,10 @@ def tile_picked_sub_mlp_relu_sub_e_kernel(tc, xT, w1, w2, gate, offs, pos1, pos2
 
         offs_t = keep.tile([P, S // LIST_ROWS], U16, name="offs_t")
         pos_t = [keep.tile([P, V // LIST_ROWS], U16, name=f"pos_t{d}") for d in range(2)]
-        plane = [own(f"plane{j}", [P, T], F32) for j in range(4)]
+        plane = [
+            spread.tile([P, T], F32, name=f"plane{j}", align_bytes=64, offset=PLANE_PLACE[j] * PLANE_PITCH)
+            for j in range(4)
+        ]
         side = own("side", [P, 4, SIDE[1] - SIDE[0]], BF16)
         w1g = [placed(f"w1g{a}", [P, 2, P, 4], BF16, AT_W1G + 2048 * a) for a in range(2)]
         picks = list(zip(LIST_CUTS[:-1], LIST_CUTS[1:]))

from contextlib import ExitStack

import concourse.mybir as mybir

K, T, S, H, N, V = 512, 2048, 1024, 512, 256, 512
P = 128

F32 = mybir.dt.float32
BF16 = mybir.dt.bfloat16
U32 = mybir.dt.uint32
U16 = mybir.dt.uint16
U8 = mybir.dt.uint8
FP8X4 = mybir.dt.float8_e4m3fn_x4

COPY = mybir.ActivationFunctionType.Copy
RELU = mybir.ActivationFunctionType.Relu
MULT = mybir.AluOpType.mult
ADD = mybir.AluOpType.add
MAX = mybir.AluOpType.max

FLOPS = 2 * S * H * K + 2 * S * N * H
LIST_ROWS = 16

PLANE_ORDER = (0, 1, 2, 3)
SIDE = (256, 704)
GPSIMD_CUTS = ((256, 480), (256, 320, 480))
SCALAR_CUTS = ((480, 704), (480, 608, 704))
LIST_CUTS = (0, 128, 256, 512, 1024)
CHUNKS = (
    (0, 128, 0, "scalar"), (128, 256, 1, "scalar"), (256, 384, 2, "vector"), (384, 512, 3, "scalar"),
    (512, 640, 4, "vector"), (640, 768, 5, "scalar"), (768, 896, 6, "scalar"), (896, 960, 0, "vector"),
    (960, 1024, 7, "scalar"),
)
PLANE_PITCH = 50 * 1024
PLANE_PLACE = (0, 2, 1, 3)
WARM_UPS = 4
W1_FIRST = 72
W1_SECOND = 80

AT_W1G = 0
AT_XC1 = AT_W1G
AT_W1R = AT_W1G + 4096
AT_XC2 = AT_W1R
AT_XC3 = AT_W1R + 1024
AT_HG0 = AT_W1R + 8192
AT_HG3 = AT_HG0
AT_W2C0 = AT_HG0 + 4096
AT_Y1 = AT_W2C0
H_PIECES = (512, 256, P, P)


def tile_picked_sub_mlp_relu_sub_e_kernel(tc, xT, w1, w2, gate, offs, pos1, pos2, out):
    nc = tc.nc
    with ExitStack() as ctx:
        keep = ctx.enter_context(tc.tile_pool(name="keep", bufs=1))
        reuse = ctx.enter_context(tc.tile_pool(name="reuse", bufs=1))
        spread = ctx.enter_context(tc.tile_pool(name="spread", bufs=1))
        psum = ctx.enter_context(tc.psum_pool(name="psum", bufs=1))

        def own(name, shape, dtype):
            return keep.tile(shape, dtype, name=name, align_bytes=64)

        def placed(name, shape, dtype, at):
            return reuse.tile(shape, dtype, name=name, align_bytes=64, offset=at)

        def take_bank(b):
            return psum.tile([P, 4, P], F32, name=f"bank{b}")

        offs_t = keep.tile([P, S // LIST_ROWS], U16, name="offs_t")
        pos_t = [keep.tile([P, V // LIST_ROWS], U16, name=f"pos_t{d}") for d in range(2)]
        plane = [
            spread.tile([P, T], F32, name=f"plane{j}", align_bytes=64, offset=PLANE_PLACE[j] * PLANE_PITCH)
            for j in range(4)
        ]
        side = own("side", [P, 4, SIDE[1] - SIDE[0]], BF16)
        w1g = [placed(f"w1g{a}", [P, 2, P, 4], BF16, AT_W1G + 2048 * a) for a in range(2)]
        picks = list(zip(LIST_CUTS[:-1], LIST_CUTS[1:]))
        xg = own("xg", [P, S, 4], BF16)
        xc = [
            own("xc0", [P, P], U32),
            placed("xc1", [P, P], U32, AT_XC1),
            placed("xc2", [P, 256], U32, AT_XC2),
            placed("xc3", [P, 512], U32, AT_XC3),
        ]
        xs = [own(f"xs{q}", [P, b - a], U8) for q, (a, b) in enumerate(picks)]
        w1r = placed("w1r", [P, 4, H], F32, AT_W1R)
        w1c = own("w1c", [P, H], U32)
        w1s = own("w1s", [P, H], U8)
        w2r = own("w2r", [P, 4, N], F32)
        w2g = own("w2g", [P, N, 4], BF16)
        w2c = [placed("w2c0", [P, P], U32, AT_W2C0), own("w2c1", [P, P], U32)]
        w2s = [own(f"w2s{m}", [P, P], U8) for m in range(2)]
        hg = [
            placed("hg0", [P, 512, 4], BF16, AT_HG0),
            own("hg1", [P, 256, 4], BF16),
            own("hg2", [P, P, 4], BF16),
            placed("hg3", [P, P, 4], BF16, AT_HG3),
        ]
        h_place = [(i, nth) for i, n in enumerate(H_PIECES) for nth in range(n // P)]
        hc = own("hc", [P, S], U32)
        hs = own("hs", [P, S], U8)
        y = [own("y0", [P, S], F32), placed("y1", [P, S], F32, AT_Y1)]
        gt = own("gt", [P, 2, V], F32)
        plain = [own(f"plain{m}", [P, V], F32) for m in range(2)]
        part = [[own(f"part{m}{d}", [P, V], F32) for d in range(2)] for m in range(2)]
        res = [own(f"res{m}", [P, V], F32) for m in range(2)]

        x4 = xT.rearrange("(p j) t -> p j t", j=4)
        w14 = w1.rearrange("(p j) c -> p j c", j=4)
        for j in PLANE_ORDER:
            nc.sync.dma_start(out=plane[j][:], in_=x4[:, j, :])
            if j == PLANE_ORDER[0]:
                nc.sync.dma_start(out=offs_t[:], in_=offs)
        nc.sync.dma_start(out=w1r[:], in_=w14)
        nc.sync.dma_start(out=w2r[:], in_=w2.rearrange("(p j) n -> p j n", j=4))
        nc.sync.dma_start(out=pos_t[0][:], in_=pos1)
        nc.sync.dma_start(out=pos_t[1][:], in_=pos2)
        nc.sync.dma_start(out=gt[:], in_=gate[:, 0:P, :].rearrange("d p v -> p d v"))

        def copy(engine, dst, src):
            if engine == "scalar":
                nc.scalar.copy(dst, src)
            else:
                nc.vector.tensor_copy(dst, src)

        def weave_w1(engine, t0, t1, a, b):
            src = w1r[:].rearrange("p j (m t) -> p m j t", t=4)[:, a:b, :, t0:t1]
            copy(engine, w1g[t0 // 2][:, :, a:b, :].rearrange("p t m j -> p m j t"), src)

        def weave(engine, dst, src):
            copy(engine, dst.rearrange("p (c i) j -> p c j i", i=4), src.rearrange("p j (c i) -> p c j i", i=4))

        def quant(words, scales, woven):
            nc.vector.quantize_mx(out=words.bitcast(FP8X4), scales=scales, in_=woven)

        def quant_x(q):
            a, b = picks[q]
            quant(xc[q][:], xs[q][:], xg[:, a:b, :].rearrange("p n j -> p (n j)"))

        def quant_w1(t):
            flat = w1g[t // 2][:, t % 2, :, :].rearrange("p m j -> p (m j)")
            quant(w1c[:, t * P : (t + 1) * P], w1s[:, t * P : (t + 1) * P], flat)

        def quant_h(a, b):
            piece, nth = h_place[a // P]
            first = nth * P + a % P
            woven = hg[piece][:, first : first + b - a, :]
            quant(hc[:, a:b], hs[:, a:b], woven.rearrange("p n j -> p (n j)"))

        def entries(list_tile, a, b):
            return list_tile[:, a // LIST_ROWS : b // LIST_ROWS]

        def gather_plane(j, a, b):
            nc.vector.tensor_copy(xg[:, a:b, j], plane[j][:].indirect(entries(offs_t, a, b)))

        h_bank = {}
        y_bank = {}

        def layer1(a, b, bank):
            h_bank[a] = take_bank(bank)[:, :, 0 : b - a]
            q = max(i for i, (lo, hi) in enumerate(picks) if lo <= a)
            cols = slice(a - picks[q][0], b - picks[q][0])
            for t in range(4):
                nc.tensor.matmul_mx(
                    out=h_bank[a][:, t, :],
                    lhsT=w1c[:, t * P : (t + 1) * P].bitcast(FP8X4),
                    lhsT_scale=w1s[:, t * P : (t + 1) * P],
                    rhs=xc[q][:, cols].bitcast(FP8X4),
                    rhs_scale=xs[q][:, cols],
                    start=True,
                    stop=True,
                )

        def relu_out(a, b, engine):
            piece, nth = h_place[a // P]
            first = nth * P + a % P
            dst = hg[piece][:, first : first + b - a, :]
            src = h_bank[a].rearrange("p t n -> p n t")
            if engine == "vector":
                nc.vector.tensor_scalar(dst, src, 0.0, None, MAX)
            else:
                nc.scalar.activation(dst, src, RELU)

        def y_bank_for(m, a, bank):
            y_bank[m, a] = take_bank(bank)[:].rearrange("p t n -> p (t n)")

        def layer2(m, first, a, b):
            nc.tensor.matmul_mx(
                out=y_bank[m, first][:, a - first : b - first],
                lhsT=w2c[m][:].bitcast(FP8X4),
                lhsT_scale=w2s[m][:],
                rhs=hc[:, a:b].bitcast(FP8X4),
                rhs_scale=hs[:, a:b],
                start=True,
                stop=True,
            )

        def y_out(engine, m, a, b):
            copy(engine, y[m][:, a:b], y_bank[m, a][:, 0 : b - a])

        def fetch_gated(m, a, b):
            nc.vector.tensor_tensor(part[m][0][:, a:b], y[m][:].indirect(entries(pos_t[0], a, b)), gt[:, 0, a:b], MULT)

        def fetch_plain(m, a, b):
            nc.scalar.activation(plain[m][:, a:b], y[m][:].indirect(entries(pos_t[1], a, b)), COPY)

        def gate_plain(m, a, b):
            nc.vector.tensor_tensor(part[m][1][:, a:b], plain[m][:, a:b], gt[:, 1, a:b], MULT)

        def finish(m, a, b):
            nc.vector.tensor_tensor(res[m][:, a:b], part[m][0][:, a:b], part[m][1][:, a:b], ADD)
            nc.sync.dma_start(out=out[m * P : (m + 1) * P, a:b], in_=res[m][:, a:b])

        def stage(j, a, b):
            staged = side[:, j, a - SIDE[0] : b - SIDE[0]]
            nc.scalar.activation(staged, plane[j][:].indirect(entries(offs_t, a, b)), COPY)

        def place(engine, u, a, b):
            dst = xg[:, a:b, 2 * u : 2 * u + 2]
            src = side[:, 2 * u : 2 * u + 2, a - SIDE[0] : b - SIDE[0]].rearrange("p e n -> p n e")
            if engine == "gpsimd":
                nc.gpsimd.tensor_scalar(dst, src, 1.0, 0.0, MULT, ADD)
            else:
                nc.scalar.copy(dst, src)

        for j in range(4):
            gather_plane(j, 0, SIDE[0])
            gather_plane(j, SIDE[1], S)
            if j % 2 == 0:
                stage(j, *SIDE)
            else:
                for engine, cuts in (("gpsimd", GPSIMD_CUTS[j // 2]), ("scalar", SCALAR_CUTS[j // 2])):
                    pieces = list(zip(cuts[:-1], cuts[1:]))
                    for a, b in pieces:
                        stage(j, a, b)
                    for a, b in pieces:
                        place(engine, j // 2, a, b)
        quant_x(0)
        warm = take_bank(7)[:].rearrange("p t n -> p (t n)")[:, 0:P]
        for rep in range(WARM_UPS):
            nc.tensor.matmul_mx(
                out=warm,
                lhsT=xc[0][:, 0:P].bitcast(FP8X4),
                lhsT_scale=xs[0][:, 0:P],
                rhs=xc[0][:].bitcast(FP8X4),
                rhs_scale=xs[0][:],
                start=True,
                stop=True,
            )
        weave_w1("vector", 0, 2, 0, W1_FIRST)
        weave_w1("scalar", 0, 2, W1_FIRST, P)
        weave_w1("vector", 2, 4, W1_SECOND, P)
        weave_w1("scalar", 2, 4, 0, W1_SECOND)
        for t in range(4):
            quant_w1(t)
            if t == 1:
                quant_x(1)
        weave("scalar", w2g[:], w2r[:])
        quant_x(2)
        quant_x(3)
        for m in range(2):
            quant(w2c[m][:], w2s[m][:], w2g[:, m * P : (m + 1) * P, :].rearrange("p n j -> p (n j)"))
        for a, b, bank, engine in CHUNKS[:7]:
            layer1(a, b, bank)
            relu_out(a, b, engine)
            if b == 384:
                quant_h(0, 256)
        for a, b, bank, engine in CHUNKS[7:]:
            layer1(a, b, bank)

        for first, bank in ((0, 1), (512, 2), (768, 5), (960, 6)):
            y_bank_for(0, first, bank)
        quant_h(256, 512)
        layer2(0, 0, 0, 512)
        quant_h(512, 768)
        for a, b, bank, engine in CHUNKS[7:]:
            relu_out(a, b, engine)
        layer2(0, 512, 512, 768)
        quant_h(768, 896)
        layer2(0, 768, 768, 896)
        quant_h(896, 960)
        layer2(0, 768, 896, 960)
        quant_h(960, 1024)
        layer2(0, 960, 960, 1024)
        y_out("scalar", 0, 0, 512)
        y_out("vector", 0, 512, 768)
        y_out("scalar", 0, 768, 960)
        y_out("scalar", 0, 960, 1024)
        for first, bank in ((0, 3), (512, 4)):
            y_bank_for(1, first, bank)
            layer2(1, first, first, first + 512)
            y_out("scalar", 1, first, first + 512)

        fetch_gated(0, 0, V)
        fetch_gated(1, 0, V)
        fetch_plain(0, 0, V)
        for a in (0, V // 2):
            fetch_plain(1, a, a + V // 2)
        gate_plain(0, 0, V)
        gate_plain(1, 0, V // 2)
        finish(0, 0, V)
        gate_plain(1, V // 2, V)
        for a in (0, V // 2):
            finish(1, a, a + V // 2)
